import numpy as np
import ml_dtypes


def mxq(x, axis, fmt="e4m3"):
    dtype, down = {"e4m3": (ml_dtypes.float8_e4m3fn, 7), "e5m2": (ml_dtypes.float8_e5m2, 14)}[fmt]
    v = np.moveaxis(np.asarray(x, np.float32).astype(ml_dtypes.bfloat16).astype(np.float64), axis, -1)
    blocks = v.reshape(v.shape[:-1] + (-1, 32))
    amax = np.abs(blocks).max(-1, keepdims=True)
    byte = np.maximum(np.where(amax > 0, np.frexp(amax)[1] - 1 + 127, 0) - down, 1)
    scale = np.exp2(byte - 127.0)
    codes = (blocks / scale).astype(np.float32).astype(dtype).astype(np.float64)
    return np.moveaxis((codes * scale).reshape(v.shape), -1, axis)


WIDE = False


def mx_kscale(k):
    if not WIDE:
        return np.ones(k)
    levels = np.array([10, -10, 5, -5, 0])
    if k % 512:
        return np.exp2(np.random.permutation(np.resize(levels, k // 32))).repeat(32)
    a = np.empty((k // 512, 16))
    for p in range(k // 512):
        a[p, :8] = np.random.permutation(np.resize(levels, 8))
        for g in range(8):
            far = levels[np.abs(levels - a[p, g]) >= 10]
            a[p, g + 8] = far[np.random.randint(len(far))]
    return np.exp2(a.ravel()).repeat(32)


def f64(x):
    return np.asarray(x).astype(np.float64)


def striped(idx):
    return np.tile(np.asarray(idx).reshape(-1, 16).T, (8, 1)).astype(np.uint16)


def unstriped(offs):
    return offs[:16].T.reshape(-1).astype(np.int64)


E2M1 = np.array([0.0, 0.5, 1.0, 1.5, 2.0, 3.0, 4.0, 6.0, -0.0, -0.5, -1.0, -1.5, -2.0, -3.0, -4.0, -6.0])


def pack_weight(w, fmt):
    k, n = w.shape
    w = f64(np.asarray(w, np.float32).astype(ml_dtypes.bfloat16)).reshape(k // 32, 32, n)
    amax = np.abs(w).max(1)
    if fmt == "e4m3":
        byte = np.frexp(amax)[1] - 1 + 127 - 7
    else:
        mant, ex = np.frexp(amax / 6.0)
        byte = np.where(mant > 0.5, ex, ex - 1) + 127
    byte = np.clip(np.where(amax > 0, byte, 1), 1, 254)
    scaled = (w * np.exp2(127.0 - byte)[:, None, :]).reshape(k, n).astype(np.float32)
    by_word = np.ascontiguousarray(scaled.reshape(k // 512, 128, 4, n).transpose(0, 1, 3, 2))
    if fmt == "e4m3":
        words = by_word.astype(ml_dtypes.float8_e4m3fn).view(np.uint8)
    else:
        c = by_word.astype(ml_dtypes.float4_e2m1fn).view(np.uint8) & 0xF
        words = (c[..., 0::2] | (c[..., 1::2] << 4)).reshape(k // 512, 128, 2 * n)
    return np.ascontiguousarray(words), np.ascontiguousarray(byte.astype(np.uint8).reshape(k // 512, 16, n))


def unpack_weight(words, scales, fmt):
    g, _, n = scales.shape
    words = np.ascontiguousarray(words).reshape(g, 128, n, -1)
    if fmt == "e4m3":
        vals = words.view(ml_dtypes.float8_e4m3fn).astype(np.float64)
    else:
        nib = np.empty((g, 128, n, 4), np.uint8)
        nib[..., 0::2] = words & 0xF
        nib[..., 1::2] = words >> 4
        vals = E2M1[nib]
    vals = vals * np.repeat(np.exp2(scales.astype(np.float64) - 127.0), 8, axis=1)[..., None]
    return vals.transpose(0, 1, 3, 2).reshape(g * 512, n)


B, N, T, D, NQ = 1, 512, 2048, 512, 512
SEG = 16


def setup_inputs():
    n = np.random.standard_normal
    idx = np.random.permutation(T)[:B * N]
    s = mx_kscale(D)[:, None]
    kp = pack_weight(n((D, T)) / s, "e4m3")
    return {
        "qT": (n((B, D, NQ)) * s * (1.00 / np.sqrt(D))).astype(np.float32),
        "k_words": kp[0],
        "k_scales": kp[1],
        "ts": np.tile(np.random.uniform(0.5, 2.0, 2048), (128, 1)).astype(np.float32),
        "hw": (np.random.uniform(-0.5, 1.0, (B, 1, NQ))).astype(np.float32),
        "offs": striped(idx),
    }


def reference(qT, k_words, k_scales, ts, hw, offs):
    idx = unstriped(offs)
    pick = lambda x, which: x[:, which].reshape(x.shape[0], B, -1).transpose(1, 0, 2)
    k = unpack_weight(k_words, k_scales, "e4m3")
    kg = pick(k, idx)
    qq = mxq(f64(qT), 1, "e4m3")
    a = kg.transpose(0, 2, 1) @ qq
    y = (np.maximum(a, 0.0) * f64(hw)).reshape(B, N, NQ // SEG, SEG).sum(-1) * pick(f64(ts), idx)[:, :1, :].transpose(0, 2, 1)
    return y

@@ -1,0 +1,187 @@
+from contextlib import ExitStack
+
+import concourse.mybir as mybir
+from concourse.masks import make_identity
+
+F32 = mybir.dt.float32
+BF16 = mybir.dt.bfloat16
+I32 = mybir.dt.int32
+U32 = mybir.dt.uint32
+U16 = mybir.dt.uint16
+U8 = mybir.dt.uint8
+FP8X4 = mybir.dt.float8_e4m3fn_x4
+ALU = mybir.AluOpType
+ACT = mybir.ActivationFunctionType
+AXIS_X = mybir.AxisListType.X
+
+P = 128
+PACK = 4
+T = 2048
+N = 512
+NQ = 512
+D = 512
+SEG = 16
+NPOS = NQ // SEG
+HALF = N // 2
+QT = NQ // P
+TS_ROW = P - 1
+SCALAR_CAST = 48
+WARM = 24
+
+FLOPS = 2 * N * NQ * D
+BYTES = 4 * D * NQ + D * T + 16 * T + 4 * T + 4 * NQ + 2 * P * (N // 16) + 4 * N * NPOS
+
+
+def tile_attend_tok_idxts_topk_kernel(tc, qT, k_words, k_scales, ts, hw, offs, out):
+    nc = tc.nc
+    with ExitStack() as ctx:
+        keep = ctx.enter_context(tc.tile_pool(name="keep", bufs=1))
+        psum = ctx.enter_context(tc.psum_pool(name="psum", bufs=1))
+
+        offsets = keep.tile([P, N // 16], U16, name="offsets")
+        q_raw = keep.tile([P, PACK, NQ], F32, name="q_raw", align_bytes=64)
+        pool_words = keep.tile([P, T], I32, name="pool_words", align_bytes=64)
+        pool_scales = keep.tile([P, T // 4], I32, name="pool_scales", align_bytes=64)
+        pool_ts = keep.tile([P, T], F32, name="pool_ts", align_bytes=64)
+        hw_cols = keep.tile([P, QT], F32, name="hw_cols")
+        ident = keep.tile([P, P], F32, name="ident", align_bytes=64)
+
+        nc.vector.memset(pool_scales[:], 0)
+        nc.vector.memset(pool_ts[0:TS_ROW, :], 0.0)
+        make_identity(nc, ident[:])
+        table_warm = keep.tile([P, 1], F32, name="table_warm")
+        nc.scalar.activation(out=table_warm[:], in_=ident[:, 0:1], func=ACT.Relu)
+
+        q_rows = qT[0].rearrange("(p t) q -> p t q", t=PACK)
+        scale_rows = k_scales[0].bitcast(I32)
+        nc.sync.dma_start(offsets[:], offs)
+        nc.sync.dma_start(out=pool_ts[TS_ROW:P, :], in_=ts[0:1, :])
+        nc.sync.dma_start(out=q_raw[:, 0:2, :], in_=q_rows[:, 0:2, :])
+        for r in range(4):
+            nc.sync.dma_start(out=pool_scales[r:P:32, :], in_=scale_rows[r:16:4, :])
+        nc.sync.dma_start(out=q_raw[:, 2:4, :], in_=q_rows[:, 2:4, :])
+        nc.sync.dma_start(out=pool_words[:], in_=k_words[0].rearrange("p n t -> p (n t)").bitcast(I32))
+        nc.gpsimd.dma_start(out=hw_cols[:], in_=hw[0, 0].rearrange("(s m) -> s m", m=QT))
+
+        ts_listed = keep.tile([P, N], F32, name="ts_listed", align_bytes=64)
+        nc.vector.tensor_copy(ts_listed[:], pool_ts[:].indirect(offsets[:]))
+        k_planes = keep.tile([P, N], U8, name="k_planes", align_bytes=64)
+        nc.vector.tensor_copy(k_planes[:], pool_scales[:].bitcast(U8).indirect(offsets[:]))
+
+        ts_bank = psum.tile([P, 4, P], F32, name="ts_bank", tag="sum00")
+        for c in range(2):
+            for u in range(2):
+                nc.tensor.transpose(ts_bank[:, 2 * c + u, :], ts_listed[:, HALF * c + u : HALF * (c + 1) : 2], ident[:])
+        ts_cols = keep.tile([P, 4], F32, name="ts_cols")
+        nc.scalar.copy(out=ts_cols[:], in_=ts_bank[:, :, TS_ROW])
+
+        warm_bank = psum.tile([P, 4, P], F32, name="warm_bank", tag="sum11")
+        for i in range(WARM):
+            nc.tensor.transpose(warm_bank[:, i % 4, :], q_raw[:, 3, P * (i % 4) : P * (i % 4 + 1)], ident[:])
+
+        q_bf = keep.tile([P, QT, P, PACK], BF16, name="q_bf", align_bytes=64)
+        src = q_raw[:].rearrange("p t (s m) -> p s t m", m=QT)
+        dst = q_bf[:].rearrange("p m s t -> p s t m")
+        nc.scalar.copy(out=dst[:, 0:SCALAR_CAST], in_=src[:, 0:SCALAR_CAST])
+        nc.vector.tensor_copy(out=dst[:, SCALAR_CAST:P], in_=src[:, SCALAR_CAST:P])
+        q_words = keep.tile([P, NQ], U32, name="q_words", align_bytes=64)
+        q_planes = keep.tile([P, NQ], U8, name="q_planes", align_bytes=64)
+        nc.vector.quantize_mx(
+            out=q_words[:].bitcast(FP8X4), scales=q_planes[:], in_=q_bf[:].rearrange("p m s t -> p (m s t)")
+        )
+
+        k_listed = []
+        for c in range(2):
+            words = keep.tile([P, HALF], U32, name="k_listed%d" % c, align_bytes=64)
+            nc.vector.tensor_copy(words[:], pool_words[:].bitcast(U32).indirect(offsets[:, 16 * c : 16 * (c + 1)]))
+            k_listed.append(words)
+
+        scores = {}
+
+        def multiply(c, ms, tag):
+            bank = psum.tile([P, len(ms), HALF], F32, name="score%d%d" % (c, ms[0]), tag=tag)
+            for i, m in enumerate(ms):
+                nc.tensor.matmul_mx(
+                    out=bank[:, i, :],
+                    lhsT=q_words[:, P * m : P * (m + 1)].bitcast(FP8X4),
+                    lhsT_scale=q_planes[:, P * m : P * (m + 1)],
+                    rhs=k_listed[c][:].bitcast(FP8X4),
+                    rhs_scale=k_planes[:, HALF * c : HALF * (c + 1)],
+                    start=True,
+                    stop=True,
+                )
+                scores[(c, m)] = bank[:, i, :].rearrange("p (s u) -> p u s", u=2)
+
+        weighted = {}
+        positive = {}
+
+        def weigh_vector(c, m):
+            w = keep.tile([P, 2, P], F32, name="weighted%d%d" % (c, m), align_bytes=64)
+            nc.vector.tensor_scalar(
+                out=w[:], in0=scores[(c, m)], scalar1=0.0, scalar2=hw_cols[:, m : m + 1], op0=ALU.max, op1=ALU.mult
+            )
+            weighted[(c, m)] = w
+
+        def relu_scalar(c, m):
+            r = keep.tile([P, 2, P], F32, name="positive%d%d" % (c, m), align_bytes=64)
+            nc.scalar.activation(out=r[:], in_=scores[(c, m)], func=ACT.Relu)
+            positive[(c, m)] = r
+
+        def weigh_scalar(c, m):
+            w = keep.tile([P, 2, P], F32, name="weighted%d%d" % (c, m), align_bytes=64)
+            nc.scalar.activation(out=w[:], in_=positive[(c, m)][:], func=ACT.Copy, scale=hw_cols[:, m : m + 1])
+            weighted[(c, m)] = w
+
+        sums = {}
+
+        def turn(c, m, first, last):
+            for u in range(2):
+                if first:
+                    sums[(c, u)] = psum.tile([P, NPOS, 4], F32, name="sums%d%d" % (c, u), tag="sum%d%d" % (c, u))
+                nc.tensor.matmul(
+                    sums[(c, u)][:].rearrange("p j h -> p (j h)"),
+                    weighted[(c, m)][:, u, :],
+                    ident[:],
+                    start=first,
+                    stop=last,
+                    is_transpose=True,
+                )
+
+        def finish(c):
+            total = keep.tile([P, 2, NPOS], F32, name="total%d" % c, align_bytes=64)
+            for u in range(2):
+                nc.vector.tensor_reduce(out=total[:, u, :], in_=sums[(c, u)][:], axis=AXIS_X, op=ALU.add)
+            result = keep.tile([P, 2, NPOS], F32, name="result%d" % c, align_bytes=64)
+            nc.vector.tensor_tensor(
+                out=result[:],
+                in0=total[:],
+                in1=ts_cols[:, 2 * c : 2 * c + 2].unsqueeze(2).to_broadcast([P, 2, NPOS]),
+                op=ALU.mult,
+            )
+            nc.sync.dma_start(
+                out=out[0, HALF * c : HALF * (c + 1), :].rearrange("(p u) j -> p u j", u=2), in_=result[:]
+            )
+
+        multiply(0, [2], "a")
+        multiply(0, [3], "b")
+        multiply(0, [0, 1], "c")
+        multiply(1, [0, 1], "d")
+        relu_scalar(0, 2)
+        relu_scalar(0, 3)
+        multiply(1, [3], "a")
+        multiply(1, [2], "b")
+        weigh_vector(0, 0)
+        weigh_vector(0, 1)
+        weigh_scalar(0, 2)
+        weigh_scalar(0, 3)
+        relu_scalar(1, 3)
+        weigh_vector(1, 0)
+        weigh_vector(1, 1)
+        weigh_vector(1, 2)
+        weigh_scalar(1, 3)
+        for i, m in enumerate((0, 1, 2, 3)):
+            turn(0, m, i == 0, i == 3)
+        for i, m in enumerate((0, 1, 2, 3)):
+            turn(1, m, i == 0, i == 3)
+        finish(0)
+        finish(1)

@@ -61,27 +61,21 @@ def tile_attend_tok_idxts_topk_kernel(tc, qT, k_words, k_scales, ts, hw, offs, o
             nc.sync.dma_start(out=pool_scales[r:P:32, :], in_=scale_rows[r:16:4, :])
         nc.sync.dma_start(out=q_raw[:, 2:4, :], in_=q_rows[:, 2:4, :])
         nc.sync.dma_start(out=pool_words[:], in_=k_words[0].rearrange("p n t -> p (n t)").bitcast(I32))
-        nc.gpsimd.dma_start(out=hw_cols[:], in_=hw[0, 0].rearrange("(s m) -> s m", m=QT))
+        nc.sync.dma_start(out=hw_cols[:], in_=hw[0, 0].rearrange("(s m) -> s m", m=QT))
 
         ts_listed = keep.tile([P, N], F32, name="ts_listed", align_bytes=64)
         nc.vector.tensor_copy(ts_listed[:], pool_ts[:].indirect(offsets[:]))
         k_planes = keep.tile([P, N], U8, name="k_planes", align_bytes=64)
         nc.vector.tensor_copy(k_planes[:], pool_scales[:].bitcast(U8).indirect(offsets[:]))
 
-        ts_bank = psum.tile([P, 4, P], F32, name="ts_bank", tag="sum00")
-        for c in range(2):
-            for u in range(2):
-                nc.tensor.transpose(ts_bank[:, 2 * c + u, :], ts_listed[:, HALF * c + u : HALF * (c + 1) : 2], ident[:])
-        ts_cols = keep.tile([P, 4], F32, name="ts_cols")
-        nc.scalar.copy(out=ts_cols[:], in_=ts_bank[:, :, TS_ROW])
-
         warm_bank = psum.tile([P, 4, P], F32, name="warm_bank", tag="sum11")
-        for i in range(WARM):
-            nc.tensor.transpose(warm_bank[:, i % 4, :], q_raw[:, 3, P * (i % 4) : P * (i % 4 + 1)], ident[:])
+        for plane, count in ((0, 10), (3, 8)):
+            for i in range(count):
+                nc.tensor.transpose(warm_bank[:, i % 4, :], q_raw[:, plane, P * (i % 4) : P * (i % 4 + 1)], ident[:])
 
         q_bf = keep.tile([P, QT, P, PACK], BF16, name="q_bf", align_bytes=64)
-        src = q_raw[:].rearrange("p t (s m) -> p s t m", m=QT)
-        dst = q_bf[:].rearrange("p m s t -> p s t m")
+        src = q_raw[:].rearrange("p t (s m) -> p s m t", m=QT)
+        dst = q_bf[:].rearrange("p m s t -> p s m t")
         nc.scalar.copy(out=dst[:, 0:SCALAR_CAST], in_=src[:, 0:SCALAR_CAST])
         nc.vector.tensor_copy(out=dst[:, SCALAR_CAST:P], in_=src[:, SCALAR_CAST:P])
         q_words = keep.tile([P, NQ], U32, name="q_words", align_bytes=64)
@@ -89,6 +83,13 @@ def tile_attend_tok_idxts_topk_kernel(tc, qT, k_words, k_scales, ts, hw, offs, o
         nc.vector.quantize_mx(
             out=q_words[:].bitcast(FP8X4), scales=q_planes[:], in_=q_bf[:].rearrange("p m s t -> p (m s t)")
         )
+
+        ts_bank = psum.tile([P, 4, P], F32, name="ts_bank", tag="sum11")
+        for c in range(2):
+            for u in range(2):
+                nc.tensor.transpose(ts_bank[:, 2 * c + u, :], ts_listed[:, HALF * c + u : HALF * (c + 1) : 2], ident[:])
+        ts_cols = keep.tile([P, 4], F32, name="ts_cols")
+        nc.scalar.copy(out=ts_cols[:], in_=ts_bank[:, :, TS_ROW])
 
         k_listed = []
         for c in range(2):

@@ -26,7 +26,6 @@ HALF = N // 2
 QT = NQ // P
 TS_ROW = P - 1
 SCALAR_CAST = 48
-WARM = 24
 
 FLOPS = 2 * N * NQ * D
 BYTES = 4 * D * NQ + D * T + 16 * T + 4 * T + 4 * NQ + 2 * P * (N // 16) + 4 * N * NPOS
@@ -46,32 +45,29 @@ def tile_attend_tok_idxts_topk_kernel(tc, qT, k_words, k_scales, ts, hw, offs, o
         hw_cols = keep.tile([P, QT], F32, name="hw_cols")
         ident = keep.tile([P, P], F32, name="ident", align_bytes=64)
 
-        nc.vector.memset(pool_scales[:], 0)
+        seed = keep.tile([P, 1], F32, name="seed")
+        nc.gpsimd.memset(seed[:], 0.0)
+        nc.gpsimd.memset(pool_scales[:], 0)
         nc.vector.memset(pool_ts[0:TS_ROW, :], 0.0)
         make_identity(nc, ident[:])
         table_warm = keep.tile([P, 1], F32, name="table_warm")
-        nc.scalar.activation(out=table_warm[:], in_=ident[:, 0:1], func=ACT.Relu)
+        nc.scalar.activation(out=table_warm[:], in_=seed[:], func=ACT.Relu)
 
         q_rows = qT[0].rearrange("(p t) q -> p t q", t=PACK)
         scale_rows = k_scales[0].bitcast(I32)
         nc.sync.dma_start(offsets[:], offs)
-        nc.sync.dma_start(out=pool_ts[TS_ROW:P, :], in_=ts[0:1, :])
+        nc.scalar.dma_start(out=pool_ts[TS_ROW:P, :], in_=ts[0:1, :])
         nc.sync.dma_start(out=q_raw[:, 0:2, :], in_=q_rows[:, 0:2, :])
         for r in range(4):
             nc.sync.dma_start(out=pool_scales[r:P:32, :], in_=scale_rows[r:16:4, :])
         nc.sync.dma_start(out=q_raw[:, 2:4, :], in_=q_rows[:, 2:4, :])
-        nc.sync.dma_start(out=pool_words[:], in_=k_words[0].rearrange("p n t -> p (n t)").bitcast(I32))
         nc.sync.dma_start(out=hw_cols[:], in_=hw[0, 0].rearrange("(s m) -> s m", m=QT))
+        nc.sync.dma_start(out=pool_words[:], in_=k_words[0].rearrange("p n t -> p (n t)").bitcast(I32))
 
         ts_listed = keep.tile([P, N], F32, name="ts_listed", align_bytes=64)
         nc.vector.tensor_copy(ts_listed[:], pool_ts[:].indirect(offsets[:]))
         k_planes = keep.tile([P, N], U8, name="k_planes", align_bytes=64)
         nc.vector.tensor_copy(k_planes[:], pool_scales[:].bitcast(U8).indirect(offsets[:]))
-
-        warm_bank = psum.tile([P, 4, P], F32, name="warm_bank", tag="sum11")
-        for plane, count in ((0, 10), (3, 8)):
-            for i in range(count):
-                nc.tensor.transpose(warm_bank[:, i % 4, :], q_raw[:, plane, P * (i % 4) : P * (i % 4 + 1)], ident[:])
 
         q_bf = keep.tile([P, QT, P, PACK], BF16, name="q_bf", align_bytes=64)
         src = q_raw[:].rearrange("p t (s m) -> p s m t", m=QT)
@@ -90,6 +86,14 @@ def tile_attend_tok_idxts_topk_kernel(tc, qT, k_words, k_scales, ts, hw, offs, o
                 nc.tensor.transpose(ts_bank[:, 2 * c + u, :], ts_listed[:, HALF * c + u : HALF * (c + 1) : 2], ident[:])
         ts_cols = keep.tile([P, 4], F32, name="ts_cols")
         nc.scalar.copy(out=ts_cols[:], in_=ts_bank[:, :, TS_ROW])
+        ts_rows = psum.tile([P, 2, P], F32, name="ts_rows", tag="sum10")
+        for u in range(2):
+            nc.tensor.transpose(ts_rows[:, u, :], ts_cols[:, 2 + u : 3 + u].to_broadcast([P, P]), ident[:])
+        both = []
+        for m in range(QT):
+            f = keep.tile([P, 2, P], F32, name="both%d" % m, align_bytes=64)
+            nc.scalar.activation(out=f[:], in_=ts_rows[:], func=ACT.Copy, scale=hw_cols[:, m : m + 1])
+            both.append(f)
 
         k_listed = []
         for c in range(2):
@@ -133,6 +137,18 @@ def tile_attend_tok_idxts_topk_kernel(tc, qT, k_words, k_scales, ts, hw, offs, o
             nc.scalar.activation(out=w[:], in_=positive[(c, m)][:], func=ACT.Copy, scale=hw_cols[:, m : m + 1])
             weighted[(c, m)] = w
 
+        def weigh_onto(c, m, onto):
+            w = keep.tile([P, 2, P], F32, name="weighted%d%d" % (c, m), align_bytes=64)
+            nc.vector.scalar_tensor_tensor(
+                out=w[:],
+                in0=positive[(c, m)][:],
+                scalar=hw_cols[:, m : m + 1],
+                in1=weighted[(c, onto)][:],
+                op0=ALU.mult,
+                op1=ALU.add,
+            )
+            weighted[(c, m)] = w
+
         sums = {}
 
         def turn(c, m, first, last):
@@ -163,26 +179,67 @@ def tile_attend_tok_idxts_topk_kernel(tc, qT, k_words, k_scales, ts, hw, offs, o
                 out=out[0, HALF * c : HALF * (c + 1), :].rearrange("(p u) j -> p u j", u=2), in_=result[:]
             )
 
-        multiply(0, [2], "a")
-        multiply(0, [3], "b")
-        multiply(0, [0, 1], "c")
-        multiply(1, [0, 1], "d")
-        relu_scalar(0, 2)
-        relu_scalar(0, 3)
-        multiply(1, [3], "a")
-        multiply(1, [2], "b")
+        def turn_bank(c, ms, tag):
+            bank = psum.tile([P, 2, NPOS, 4], F32, name="sums%d" % c, tag=tag)
+            for u in range(2):
+                for i, m in enumerate(ms):
+                    nc.tensor.matmul(
+                        bank[:, u].rearrange("p j h -> p (j h)"),
+                        weighted[(c, m)][:, u, :],
+                        ident[:],
+                        start=(i == 0),
+                        stop=(i == len(ms) - 1),
+                        is_transpose=True,
+                    )
+            return bank
+
+        def finish_bank(c, bank):
+            total = keep.tile([P, 2, NPOS], F32, name="total%d" % c, align_bytes=64)
+            nc.vector.tensor_reduce(out=total[:], in_=bank[:], axis=AXIS_X, op=ALU.add)
+            result = keep.tile([P, 2, NPOS], F32, name="result%d" % c, align_bytes=64)
+            nc.vector.tensor_tensor(
+                out=result[:],
+                in0=total[:],
+                in1=ts_cols[:, 2 * c : 2 * c + 2].unsqueeze(2).to_broadcast([P, 2, NPOS]),
+                op=ALU.mult,
+            )
+            nc.sync.dma_start(
+                out=out[0, HALF * c : HALF * (c + 1), :].rearrange("(p u) j -> p u j", u=2), in_=result[:]
+            )
+
+        def weigh_both(m):
+            w = keep.tile([P, 2, P], F32, name="weighted1%d" % m, align_bytes=64)
+            nc.vector.scalar_tensor_tensor(
+                out=w[:], in0=scores[(1, m)], scalar=0.0, in1=both[m][:], op0=ALU.max, op1=ALU.mult
+            )
+            weighted[(1, m)] = w
+
+        def finish_scaled(c):
+            result = keep.tile([P, 2, NPOS], F32, name="result%d" % c, align_bytes=64)
+            for u in range(2):
+                nc.vector.tensor_reduce(out=result[:, u, :], in_=sums[(c, u)][:], axis=AXIS_X, op=ALU.add)
+            nc.sync.dma_start(
+                out=out[0, HALF * c : HALF * (c + 1), :].rearrange("(p u) j -> p u j", u=2), in_=result[:]
+            )
+
+        multiply(0, [0], "a")
+        multiply(0, [1], "b")
+        multiply(0, [2], "c")
+        multiply(0, [3], "d")
+        multiply(1, [0], "e")
         weigh_vector(0, 0)
-        weigh_vector(0, 1)
-        weigh_scalar(0, 2)
+        relu_scalar(0, 1)
+        multiply(1, [1], "a")
+        weigh_vector(0, 2)
+        relu_scalar(0, 3)
+        multiply(1, [2], "b")
+        multiply(1, [3], "c")
+        weigh_onto(0, 1, 0)
         weigh_scalar(0, 3)
-        relu_scalar(1, 3)
-        weigh_vector(1, 0)
-        weigh_vector(1, 1)
-        weigh_vector(1, 2)
-        weigh_scalar(1, 3)
-        for i, m in enumerate((0, 1, 2, 3)):
-            turn(0, m, i == 0, i == 3)
-        for i, m in enumerate((0, 1, 2, 3)):
-            turn(1, m, i == 0, i == 3)
-        finish(0)
-        finish(1)
+        for m in range(QT):
+            weigh_both(m)
+        bank0 = turn_bank(0, [1, 2, 3], "sum00")
+        for m in range(QT):
+            turn(1, m, m == 0, m == 3)
+        finish_bank(0, bank0)
+        finish_scaled(1)

@@ -222,6 +222,11 @@ def tile_attend_tok_idxts_topk_kernel(tc, qT, k_words, k_scales, ts, hw, offs, o
                 out=out[0, HALF * c : HALF * (c + 1), :].rearrange("(p u) j -> p u j", u=2), in_=result[:]
             )
 
+        def weigh_both_gpsimd(m):
+            w = keep.tile([P, 2, P], F32, name="weighted1%d" % m, align_bytes=64)
+            nc.gpsimd.tensor_tensor(out=w[:], in0=positive[(1, m)][:], in1=both[m][:], op=ALU.mult)
+            weighted[(1, m)] = w
+
         multiply(0, [0], "a")
         multiply(0, [1], "b")
         multiply(0, [2], "c")
@@ -232,14 +237,23 @@ def tile_attend_tok_idxts_topk_kernel(tc, qT, k_words, k_scales, ts, hw, offs, o
         multiply(1, [1], "a")
         weigh_vector(0, 2)
         relu_scalar(0, 3)
+        relu_scalar(1, 0)
         multiply(1, [2], "b")
         multiply(1, [3], "c")
         weigh_onto(0, 1, 0)
+
         weigh_scalar(0, 3)
-        for m in range(QT):
-            weigh_both(m)
+        weigh_both_gpsimd(0)
+        weigh_both(1)
+        weigh_both(2)
+        w = keep.tile([P, 2, P], F32, name="weighted13", align_bytes=64)
+        for u in range(2):
+            nc.vector.scalar_tensor_tensor(
+                out=w[:, u], in0=scores[(1, 3)][:, u], scalar=0.0, in1=both[3][:, u], op0=ALU.max, op1=ALU.mult
+            )
+        weighted[(1, 3)] = w
         bank0 = turn_bank(0, [1, 2, 3], "sum00")
-        for m in range(QT):
-            turn(1, m, m == 0, m == 3)
+        for i, m in enumerate((1, 2, 0, 3)):
+            turn(1, m, i == 0, i == 3)
         finish_bank(0, bank0)
         finish_scaled(1)

@@ -95,6 +95,17 @@ def tile_attend_tok_idxts_topk_kernel(tc, qT, k_words, k_scales, ts, hw, offs, o
             nc.scalar.activation(out=f[:], in_=ts_rows[:], func=ACT.Copy, scale=hw_cols[:, m : m + 1])
             both.append(f)
 
+        warm = psum.tile([P, NQ], F32, name="warm", tag="sum11")
+        nc.tensor.matmul_mx(
+            out=warm[:],
+            lhsT=q_words[:, 0:P].bitcast(FP8X4),
+            lhsT_scale=q_planes[:, 0:P],
+            rhs=q_words[:].bitcast(FP8X4),
+            rhs_scale=q_planes[:],
+            start=True,
+            stop=True,
+        )
+
         k_listed = []
         for c in range(2):
             words = keep.tile([P, HALF], U32, name="k_listed%d" % c, align_bytes=64)

@@ -24,8 +24,10 @@ SEG = 16
 NPOS = NQ // SEG
 HALF = N // 2
 QT = NQ // P
+HEADS_LEFT = SEG // QT
+LIST_COLS = HALF // 16
 TS_ROW = P - 1
-SCALAR_CAST = 48
+SCALAR_CAST = 56
 
 FLOPS = 2 * N * NQ * D
 BYTES = 4 * D * NQ + D * T + 16 * T + 4 * T + 4 * NQ + 2 * P * (N // 16) + 4 * N * NPOS
@@ -45,13 +47,13 @@ def tile_attend_tok_idxts_topk_kernel(tc, qT, k_words, k_scales, ts, hw, offs, o
         hw_cols = keep.tile([P, QT], F32, name="hw_cols")
         ident = keep.tile([P, P], F32, name="ident", align_bytes=64)
 
-        seed = keep.tile([P, 1], F32, name="seed")
-        nc.gpsimd.memset(seed[:], 0.0)
+        table_seed = keep.tile([P, 1], F32, name="table_seed")
+        nc.gpsimd.memset(table_seed[:], 0.0)
         nc.gpsimd.memset(pool_scales[:], 0)
         nc.vector.memset(pool_ts[0:TS_ROW, :], 0.0)
         make_identity(nc, ident[:])
         table_warm = keep.tile([P, 1], F32, name="table_warm")
-        nc.scalar.activation(out=table_warm[:], in_=seed[:], func=ACT.Relu)
+        nc.scalar.activation(out=table_warm[:], in_=table_seed[:], func=ACT.Relu)
 
         q_rows = qT[0].rearrange("(p t) q -> p t q", t=PACK)
         scale_rows = k_scales[0].bitcast(I32)
@@ -70,34 +72,35 @@ def tile_attend_tok_idxts_topk_kernel(tc, qT, k_words, k_scales, ts, hw, offs, o
         nc.vector.tensor_copy(k_planes[:], pool_scales[:].bitcast(U8).indirect(offsets[:]))
 
         q_bf = keep.tile([P, QT, P, PACK], BF16, name="q_bf", align_bytes=64)
-        src = q_raw[:].rearrange("p t (s m) -> p s m t", m=QT)
-        dst = q_bf[:].rearrange("p m s t -> p s m t")
-        nc.scalar.copy(out=dst[:, 0:SCALAR_CAST], in_=src[:, 0:SCALAR_CAST])
-        nc.vector.tensor_copy(out=dst[:, SCALAR_CAST:P], in_=src[:, SCALAR_CAST:P])
+        cast_in = q_raw[:].rearrange("p t (s m) -> p s m t", m=QT)
+        cast_out = q_bf[:].rearrange("p m s t -> p s m t")
+        nc.scalar.copy(out=cast_out[:, 0:SCALAR_CAST], in_=cast_in[:, 0:SCALAR_CAST])
+        nc.vector.tensor_copy(out=cast_out[:, SCALAR_CAST:P], in_=cast_in[:, SCALAR_CAST:P])
         q_words = keep.tile([P, NQ], U32, name="q_words", align_bytes=64)
         q_planes = keep.tile([P, NQ], U8, name="q_planes", align_bytes=64)
         nc.vector.quantize_mx(
             out=q_words[:].bitcast(FP8X4), scales=q_planes[:], in_=q_bf[:].rearrange("p m s t -> p (m s t)")
         )
 
-        ts_bank = psum.tile([P, 4, P], F32, name="ts_bank", tag="sum11")
+        ts_bank = psum.tile([P, 4, P], F32, name="ts_bank", tag="sum2")
         for c in range(2):
             for u in range(2):
                 nc.tensor.transpose(ts_bank[:, 2 * c + u, :], ts_listed[:, HALF * c + u : HALF * (c + 1) : 2], ident[:])
         ts_cols = keep.tile([P, 4], F32, name="ts_cols")
         nc.scalar.copy(out=ts_cols[:], in_=ts_bank[:, :, TS_ROW])
-        ts_rows = psum.tile([P, 2, P], F32, name="ts_rows", tag="sum10")
+
+        ts_rows = psum.tile([P, 2, P], F32, name="ts_rows", tag="sum1")
         for u in range(2):
             nc.tensor.transpose(ts_rows[:, u, :], ts_cols[:, 2 + u : 3 + u].to_broadcast([P, P]), ident[:])
-        both = []
+        hw_ts = []
         for m in range(QT):
-            f = keep.tile([P, 2, P], F32, name="both%d" % m, align_bytes=64)
-            nc.scalar.activation(out=f[:], in_=ts_rows[:], func=ACT.Copy, scale=hw_cols[:, m : m + 1])
-            both.append(f)
+            factor = keep.tile([P, 2, P], F32, name="hw_ts%d" % m, align_bytes=64)
+            nc.scalar.activation(out=factor[:], in_=ts_rows[:], func=ACT.Copy, scale=hw_cols[:, m : m + 1])
+            hw_ts.append(factor)
 
-        warm = psum.tile([P, NQ], F32, name="warm", tag="sum11")
+        pe_warm = psum.tile([P, NQ], F32, name="pe_warm", tag="sum2")
         nc.tensor.matmul_mx(
-            out=warm[:],
+            out=pe_warm[:],
             lhsT=q_words[:, 0:P].bitcast(FP8X4),
             lhsT_scale=q_planes[:, 0:P],
             rhs=q_words[:].bitcast(FP8X4),
@@ -109,162 +112,112 @@ def tile_attend_tok_idxts_topk_kernel(tc, qT, k_words, k_scales, ts, hw, offs, o
         k_listed = []
         for c in range(2):
             words = keep.tile([P, HALF], U32, name="k_listed%d" % c, align_bytes=64)
-            nc.vector.tensor_copy(words[:], pool_words[:].bitcast(U32).indirect(offsets[:, 16 * c : 16 * (c + 1)]))
+            entries = offsets[:, LIST_COLS * c : LIST_COLS * (c + 1)]
+            nc.vector.tensor_copy(words[:], pool_words[:].bitcast(U32).indirect(entries))
             k_listed.append(words)
 
         scores = {}
-
-        def multiply(c, ms, tag):
-            bank = psum.tile([P, len(ms), HALF], F32, name="score%d%d" % (c, ms[0]), tag=tag)
-            for i, m in enumerate(ms):
-                nc.tensor.matmul_mx(
-                    out=bank[:, i, :],
-                    lhsT=q_words[:, P * m : P * (m + 1)].bitcast(FP8X4),
-                    lhsT_scale=q_planes[:, P * m : P * (m + 1)],
-                    rhs=k_listed[c][:].bitcast(FP8X4),
-                    rhs_scale=k_planes[:, HALF * c : HALF * (c + 1)],
-                    start=True,
-                    stop=True,
-                )
-                scores[(c, m)] = bank[:, i, :].rearrange("p (s u) -> p u s", u=2)
-
-        weighted = {}
         positive = {}
-
-        def weigh_vector(c, m):
-            w = keep.tile([P, 2, P], F32, name="weighted%d%d" % (c, m), align_bytes=64)
-            nc.vector.tensor_scalar(
-                out=w[:], in0=scores[(c, m)], scalar1=0.0, scalar2=hw_cols[:, m : m + 1], op0=ALU.max, op1=ALU.mult
-            )
-            weighted[(c, m)] = w
-
-        def relu_scalar(c, m):
-            r = keep.tile([P, 2, P], F32, name="positive%d%d" % (c, m), align_bytes=64)
-            nc.scalar.activation(out=r[:], in_=scores[(c, m)], func=ACT.Relu)
-            positive[(c, m)] = r
-
-        def weigh_scalar(c, m):
-            w = keep.tile([P, 2, P], F32, name="weighted%d%d" % (c, m), align_bytes=64)
-            nc.scalar.activation(out=w[:], in_=positive[(c, m)][:], func=ACT.Copy, scale=hw_cols[:, m : m + 1])
-            weighted[(c, m)] = w
-
-        def weigh_onto(c, m, onto):
-            w = keep.tile([P, 2, P], F32, name="weighted%d%d" % (c, m), align_bytes=64)
-            nc.vector.scalar_tensor_tensor(
-                out=w[:],
-                in0=positive[(c, m)][:],
-                scalar=hw_cols[:, m : m + 1],
-                in1=weighted[(c, onto)][:],
-                op0=ALU.mult,
-                op1=ALU.add,
-            )
-            weighted[(c, m)] = w
-
+        weighted = {}
         sums = {}
 
-        def turn(c, m, first, last):
-            for u in range(2):
-                if first:
-                    sums[(c, u)] = psum.tile([P, NPOS, 4], F32, name="sums%d%d" % (c, u), tag="sum%d%d" % (c, u))
-                nc.tensor.matmul(
-                    sums[(c, u)][:].rearrange("p j h -> p (j h)"),
-                    weighted[(c, m)][:, u, :],
-                    ident[:],
-                    start=first,
-                    stop=last,
-                    is_transpose=True,
-                )
-
-        def finish(c):
-            total = keep.tile([P, 2, NPOS], F32, name="total%d" % c, align_bytes=64)
-            for u in range(2):
-                nc.vector.tensor_reduce(out=total[:, u, :], in_=sums[(c, u)][:], axis=AXIS_X, op=ALU.add)
-            result = keep.tile([P, 2, NPOS], F32, name="result%d" % c, align_bytes=64)
-            nc.vector.tensor_tensor(
-                out=result[:],
-                in0=total[:],
-                in1=ts_cols[:, 2 * c : 2 * c + 2].unsqueeze(2).to_broadcast([P, 2, NPOS]),
-                op=ALU.mult,
+        def multiply(c, m, tag):
+            bank = psum.tile([P, HALF], F32, name="scores%d%d" % (c, m), tag=tag)
+            nc.tensor.matmul_mx(
+                out=bank[:],
+                lhsT=q_words[:, P * m : P * (m + 1)].bitcast(FP8X4),
+                lhsT_scale=q_planes[:, P * m : P * (m + 1)],
+                rhs=k_listed[c][:].bitcast(FP8X4),
+                rhs_scale=k_planes[:, HALF * c : HALF * (c + 1)],
+                start=True,
+                stop=True,
             )
-            nc.sync.dma_start(
-                out=out[0, HALF * c : HALF * (c + 1), :].rearrange("(p u) j -> p u j", u=2), in_=result[:]
+            scores[(c, m)] = bank[:].rearrange("s (p u) -> s u p", u=2)
+
+        def new_weighted(c, m):
+            tile = keep.tile([P, 2, P], F32, name="weighted%d%d" % (c, m), align_bytes=64)
+            weighted[(c, m)] = tile
+            return tile
+
+        def relu_on_scalar(c, m):
+            tile = keep.tile([P, 2, P], F32, name="positive%d%d" % (c, m), align_bytes=64)
+            nc.scalar.activation(out=tile[:], in_=scores[(c, m)], func=ACT.Relu)
+            positive[(c, m)] = tile
+
+        def relu_times_hw_on_vector(m):
+            nc.vector.tensor_scalar(
+                out=new_weighted(0, m)[:],
+                in0=scores[(0, m)],
+                scalar1=0.0,
+                scalar2=hw_cols[:, m : m + 1],
+                op0=ALU.max,
+                op1=ALU.mult,
             )
 
-        def turn_bank(c, ms, tag):
-            bank = psum.tile([P, 2, NPOS, 4], F32, name="sums%d" % c, tag=tag)
-            for u in range(2):
-                for i, m in enumerate(ms):
+        def relu_times_hw_ts_on_vector(target, source, factor):
+            nc.vector.scalar_tensor_tensor(out=target, in0=source, scalar=0.0, in1=factor, op0=ALU.max, op1=ALU.mult)
+
+        def turn_and_add(c, tiles, tags):
+            for i, m in enumerate(tiles):
+                for u in range(2):
+                    if i == 0:
+                        sums[(c, u)] = psum.tile([P, NPOS, HEADS_LEFT], F32, name="sums%d%d" % (c, u), tag=tags[u])
                     nc.tensor.matmul(
-                        bank[:, u].rearrange("p j h -> p (j h)"),
+                        sums[(c, u)][:].rearrange("p j a -> p (j a)"),
                         weighted[(c, m)][:, u, :],
                         ident[:],
                         start=(i == 0),
-                        stop=(i == len(ms) - 1),
+                        stop=(i == len(tiles) - 1),
                         is_transpose=True,
                     )
-            return bank
 
-        def finish_bank(c, bank):
-            total = keep.tile([P, 2, NPOS], F32, name="total%d" % c, align_bytes=64)
-            nc.vector.tensor_reduce(out=total[:], in_=bank[:], axis=AXIS_X, op=ALU.add)
-            result = keep.tile([P, 2, NPOS], F32, name="result%d" % c, align_bytes=64)
-            nc.vector.tensor_tensor(
-                out=result[:],
-                in0=total[:],
-                in1=ts_cols[:, 2 * c : 2 * c + 2].unsqueeze(2).to_broadcast([P, 2, NPOS]),
-                op=ALU.mult,
-            )
-            nc.sync.dma_start(
-                out=out[0, HALF * c : HALF * (c + 1), :].rearrange("(p u) j -> p u j", u=2), in_=result[:]
-            )
-
-        def weigh_both(m):
-            w = keep.tile([P, 2, P], F32, name="weighted1%d" % m, align_bytes=64)
-            nc.vector.scalar_tensor_tensor(
-                out=w[:], in0=scores[(1, m)], scalar=0.0, in1=both[m][:], op0=ALU.max, op1=ALU.mult
-            )
-            weighted[(1, m)] = w
-
-        def finish_scaled(c):
-            result = keep.tile([P, 2, NPOS], F32, name="result%d" % c, align_bytes=64)
+        def add_heads(c, target):
             for u in range(2):
-                nc.vector.tensor_reduce(out=result[:, u, :], in_=sums[(c, u)][:], axis=AXIS_X, op=ALU.add)
+                nc.vector.tensor_reduce(out=target[:, u, :], in_=sums[(c, u)][:], axis=AXIS_X, op=ALU.add)
+
+        def store(c, result):
             nc.sync.dma_start(
                 out=out[0, HALF * c : HALF * (c + 1), :].rearrange("(p u) j -> p u j", u=2), in_=result[:]
             )
 
-        def weigh_both_gpsimd(m):
-            w = keep.tile([P, 2, P], F32, name="weighted1%d" % m, align_bytes=64)
-            nc.gpsimd.tensor_tensor(out=w[:], in0=positive[(1, m)][:], in1=both[m][:], op=ALU.mult)
-            weighted[(1, m)] = w
+        for m in range(QT):
+            multiply(0, m, "score%d" % m)
+        multiply(1, 0, "score4")
+        relu_times_hw_on_vector(0)
+        relu_on_scalar(0, 1)
+        multiply(1, 1, "score0")
+        relu_times_hw_on_vector(2)
+        relu_on_scalar(0, 3)
+        relu_on_scalar(1, 0)
+        multiply(1, 2, "score1")
+        multiply(1, 3, "score2")
 
-        multiply(0, [0], "a")
-        multiply(0, [1], "b")
-        multiply(0, [2], "c")
-        multiply(0, [3], "d")
-        multiply(1, [0], "e")
-        weigh_vector(0, 0)
-        relu_scalar(0, 1)
-        multiply(1, [1], "a")
-        weigh_vector(0, 2)
-        relu_scalar(0, 3)
-        relu_scalar(1, 0)
-        multiply(1, [2], "b")
-        multiply(1, [3], "c")
-        weigh_onto(0, 1, 0)
-
-        weigh_scalar(0, 3)
-        weigh_both_gpsimd(0)
-        weigh_both(1)
-        weigh_both(2)
-        w = keep.tile([P, 2, P], F32, name="weighted13", align_bytes=64)
+        nc.vector.scalar_tensor_tensor(
+            out=new_weighted(0, 1)[:],
+            in0=positive[(0, 1)][:],
+            scalar=hw_cols[:, 1:2],
+            in1=weighted[(0, 0)][:],
+            op0=ALU.mult,
+            op1=ALU.add,
+        )
+        nc.scalar.activation(out=new_weighted(0, 3)[:], in_=positive[(0, 3)][:], func=ACT.Copy, scale=hw_cols[:, 3:4])
+        nc.gpsimd.tensor_tensor(out=new_weighted(1, 0)[:], in0=positive[(1, 0)][:], in1=hw_ts[0][:], op=ALU.mult)
+        for m in (1, 2):
+            relu_times_hw_ts_on_vector(new_weighted(1, m)[:], scores[(1, m)], hw_ts[m][:])
+        last = new_weighted(1, 3)
         for u in range(2):
-            nc.vector.scalar_tensor_tensor(
-                out=w[:, u], in0=scores[(1, 3)][:, u], scalar=0.0, in1=both[3][:, u], op0=ALU.max, op1=ALU.mult
-            )
-        weighted[(1, 3)] = w
-        bank0 = turn_bank(0, [1, 2, 3], "sum00")
-        for i, m in enumerate((1, 2, 0, 3)):
-            turn(1, m, i == 0, i == 3)
-        finish_bank(0, bank0)
-        finish_scaled(1)
+            relu_times_hw_ts_on_vector(last[:, u], scores[(1, 3)][:, u], hw_ts[3][:, u])
+
+        turn_and_add(0, (2, 1, 3), ("sum0", "score3"))
+        turn_and_add(1, (1, 2, 0, 3), ("sum1", "sum2"))
+
+        total0 = keep.tile([P, 2, NPOS], F32, name="total0", align_bytes=64)
+        add_heads(0, total0)
+        result0 = keep.tile([P, 2, NPOS], F32, name="result0", align_bytes=64)
+        for u in range(2):
+            nc.scalar.activation(out=result0[:, u, :], in_=total0[:, u, :], func=ACT.Copy, scale=ts_cols[:, u : u + 1])
+        store(0, result0)
+
+        result1 = keep.tile([P, 2, NPOS], F32, name="result1", align_bytes=64)
+        add_heads(1, result1)
+        store(1, result1)

@@ -27,7 +27,7 @@ QT = NQ // P
 HEADS_LEFT = SEG // QT
 LIST_COLS = HALF // 16
 TS_ROW = P - 1
-SCALAR_CAST = 56
+SCALAR_CAST = 68
 
 FLOPS = 2 * N * NQ * D
 BYTES = 4 * D * NQ + D * T + 16 * T + 4 * T + 4 * NQ + 2 * P * (N // 16) + 4 * N * NPOS
@@ -40,7 +40,7 @@ def tile_attend_tok_idxts_topk_kernel(tc, qT, k_words, k_scales, ts, hw, offs, o
         psum = ctx.enter_context(tc.psum_pool(name="psum", bufs=1))
 
         offsets = keep.tile([P, N // 16], U16, name="offsets")
-        q_raw = keep.tile([P, PACK, NQ], F32, name="q_raw", align_bytes=64)
+        q_raw = keep.tile([P, PACK, NQ], F32, name="q_raw", tag="q_raw_then_ts_cols", align_bytes=64)
         pool_words = keep.tile([P, T], I32, name="pool_words", align_bytes=64)
         pool_scales = keep.tile([P, T // 4], I32, name="pool_scales", align_bytes=64)
         pool_ts = keep.tile([P, T], F32, name="pool_ts", align_bytes=64)
@@ -48,8 +48,10 @@ def tile_attend_tok_idxts_topk_kernel(tc, qT, k_words, k_scales, ts, hw, offs, o
         ident = keep.tile([P, P], F32, name="ident", align_bytes=64)
 
         table_seed = keep.tile([P, 1], F32, name="table_seed")
-        nc.gpsimd.memset(table_seed[:], 0.0)
+        nc.vector.memset(table_seed[:], 0.0)
         nc.gpsimd.memset(pool_scales[:], 0)
+        k_planes = keep.tile([P, N], U8, name="k_planes", align_bytes=64)
+        nc.gpsimd.memset(k_planes[:].bitcast(I32), 0)
         nc.vector.memset(pool_ts[0:TS_ROW, :], 0.0)
         make_identity(nc, ident[:])
         table_warm = keep.tile([P, 1], F32, name="table_warm")
@@ -58,18 +60,22 @@ def tile_attend_tok_idxts_topk_kernel(tc, qT, k_words, k_scales, ts, hw, offs, o
         q_rows = qT[0].rearrange("(p t) q -> p t q", t=PACK)
         scale_rows = k_scales[0].bitcast(I32)
         nc.sync.dma_start(offsets[:], offs)
-        nc.scalar.dma_start(out=pool_ts[TS_ROW:P, :], in_=ts[0:1, :])
-        nc.sync.dma_start(out=q_raw[:, 0:2, :], in_=q_rows[:, 0:2, :])
-        for r in range(4):
-            nc.sync.dma_start(out=pool_scales[r:P:32, :], in_=scale_rows[r:16:4, :])
-        nc.sync.dma_start(out=q_raw[:, 2:4, :], in_=q_rows[:, 2:4, :])
+        nc.sync.dma_start(out=q_raw[:, 0:1, :], in_=q_rows[:, 0:1, :])
+        nc.sync.dma_start(out=pool_scales[0:P:8, :], in_=scale_rows)
+        nc.sync.dma_start(out=pool_ts[TS_ROW:P, :], in_=ts[0:1, :])
+        nc.sync.dma_start(out=q_raw[:, 1:4, :], in_=q_rows[:, 1:4, :])
         nc.sync.dma_start(out=hw_cols[:], in_=hw[0, 0].rearrange("(s m) -> s m", m=QT))
         nc.sync.dma_start(out=pool_words[:], in_=k_words[0].rearrange("p n t -> p (n t)").bitcast(I32))
 
-        ts_listed = keep.tile([P, N], F32, name="ts_listed", align_bytes=64)
-        nc.vector.tensor_copy(ts_listed[:], pool_ts[:].indirect(offsets[:]))
-        k_planes = keep.tile([P, N], U8, name="k_planes", align_bytes=64)
-        nc.vector.tensor_copy(k_planes[:], pool_scales[:].bitcast(U8).indirect(offsets[:]))
+        scales_listed = keep.tile([P, N], U8, name="scales_listed", align_bytes=64)
+        nc.vector.tensor_copy(scales_listed[:], pool_scales[:].bitcast(U8).indirect(offsets[:]))
+        for r in range(4):
+            nc.sync.dma_start(out=k_planes[:].bitcast(I32)[r:P:32, :], in_=scales_listed[:].bitcast(I32)[8 * r : P : 32, :])
+        ts_listed = {}
+        for c in (1, 0):
+            ts_listed[c] = keep.tile([P, HALF], F32, name="ts_listed%d" % c, align_bytes=64)
+            entries = offsets[:, LIST_COLS * c : LIST_COLS * (c + 1)]
+            nc.vector.tensor_copy(ts_listed[c][:], pool_ts[:].indirect(entries))
 
         q_bf = keep.tile([P, QT, P, PACK], BF16, name="q_bf", align_bytes=64)
         cast_in = q_raw[:].rearrange("p t (s m) -> p s m t", m=QT)
@@ -83,10 +89,10 @@ def tile_attend_tok_idxts_topk_kernel(tc, qT, k_words, k_scales, ts, hw, offs, o
         )
 
         ts_bank = psum.tile([P, 4, P], F32, name="ts_bank", tag="sum2")
-        for c in range(2):
+        for c in (1, 0):
             for u in range(2):
-                nc.tensor.transpose(ts_bank[:, 2 * c + u, :], ts_listed[:, HALF * c + u : HALF * (c + 1) : 2], ident[:])
-        ts_cols = keep.tile([P, 4], F32, name="ts_cols")
+                nc.tensor.transpose(ts_bank[:, 2 * c + u, :], ts_listed[c][:, u:HALF:2], ident[:])
+        ts_cols = keep.tile([P, 4], F32, name="ts_cols", tag="q_raw_then_ts_cols", align_bytes=64)
         nc.scalar.copy(out=ts_cols[:], in_=ts_bank[:, :, TS_ROW])
 
         ts_rows = psum.tile([P, 2, P], F32, name="ts_rows", tag="sum1")

@@ -27,7 +27,8 @@ QT = NQ // P
 HEADS_LEFT = SEG // QT
 LIST_COLS = HALF // 16
 TS_ROW = P - 1
-SCALAR_CAST = 68
+SCALAR_CAST = 64
+VECTOR_ZEROES = 1376
 
 FLOPS = 2 * N * NQ * D
 BYTES = 4 * D * NQ + D * T + 16 * T + 4 * T + 4 * NQ + 2 * P * (N // 16) + 4 * N * NPOS
@@ -40,19 +41,21 @@ def tile_attend_tok_idxts_topk_kernel(tc, qT, k_words, k_scales, ts, hw, offs, o
         psum = ctx.enter_context(tc.psum_pool(name="psum", bufs=1))
 
         offsets = keep.tile([P, N // 16], U16, name="offsets")
-        q_raw = keep.tile([P, PACK, NQ], F32, name="q_raw", tag="q_raw_then_ts_cols", align_bytes=64)
+        q_raw = keep.tile([P, PACK, NQ], F32, name="q_raw", align_bytes=64)
         pool_words = keep.tile([P, T], I32, name="pool_words", align_bytes=64)
-        pool_scales = keep.tile([P, T // 4], I32, name="pool_scales", align_bytes=64)
+        pool_scales = keep.tile([P, T // 4], I32, name="pool_scales", tag="scales_then_ts", align_bytes=64)
         pool_ts = keep.tile([P, T], F32, name="pool_ts", align_bytes=64)
         hw_cols = keep.tile([P, QT], F32, name="hw_cols")
         ident = keep.tile([P, P], F32, name="ident", align_bytes=64)
 
         table_seed = keep.tile([P, 1], F32, name="table_seed")
-        nc.vector.memset(table_seed[:], 0.0)
-        nc.gpsimd.memset(pool_scales[:], 0)
+        nc.vector.memset(pool_scales[:, 0 : T // 8], 0)
+        nc.gpsimd.memset(pool_scales[:, T // 8 : T // 4], 0)
+        nc.gpsimd.memset(table_seed[:], 0.0)
+        nc.gpsimd.memset(pool_ts[0:TS_ROW, VECTOR_ZEROES:T], 0.0)
         k_planes = keep.tile([P, N], U8, name="k_planes", align_bytes=64)
         nc.gpsimd.memset(k_planes[:].bitcast(I32), 0)
-        nc.vector.memset(pool_ts[0:TS_ROW, :], 0.0)
+        nc.vector.memset(pool_ts[0:TS_ROW, 0:VECTOR_ZEROES], 0.0)
         make_identity(nc, ident[:])
         table_warm = keep.tile([P, 1], F32, name="table_warm")
         nc.scalar.activation(out=table_warm[:], in_=table_seed[:], func=ACT.Relu)
@@ -60,22 +63,40 @@ def tile_attend_tok_idxts_topk_kernel(tc, qT, k_words, k_scales, ts, hw, offs, o
         q_rows = qT[0].rearrange("(p t) q -> p t q", t=PACK)
         scale_rows = k_scales[0].bitcast(I32)
         nc.sync.dma_start(offsets[:], offs)
+        nc.sync.dma_start(out=pool_ts[TS_ROW:P, :], in_=ts[0:1, :])
         nc.sync.dma_start(out=q_raw[:, 0:1, :], in_=q_rows[:, 0:1, :])
         nc.sync.dma_start(out=pool_scales[0:P:8, :], in_=scale_rows)
-        nc.sync.dma_start(out=pool_ts[TS_ROW:P, :], in_=ts[0:1, :])
         nc.sync.dma_start(out=q_raw[:, 1:4, :], in_=q_rows[:, 1:4, :])
         nc.sync.dma_start(out=hw_cols[:], in_=hw[0, 0].rearrange("(s m) -> s m", m=QT))
         nc.sync.dma_start(out=pool_words[:], in_=k_words[0].rearrange("p n t -> p (n t)").bitcast(I32))
 
+        ts_listed = {}
+
+        def gather_ts(c, tag):
+            ts_listed[c] = keep.tile([P, HALF], F32, name="ts_listed%d" % c, tag=tag, align_bytes=64)
+            entries = offsets[:, LIST_COLS * c : LIST_COLS * (c + 1)]
+            nc.vector.tensor_copy(ts_listed[c][:], pool_ts[:].indirect(entries))
+
+        gather_ts(1, "ts_listed1")
         scales_listed = keep.tile([P, N], U8, name="scales_listed", align_bytes=64)
         nc.vector.tensor_copy(scales_listed[:], pool_scales[:].bitcast(U8).indirect(offsets[:]))
         for r in range(4):
             nc.sync.dma_start(out=k_planes[:].bitcast(I32)[r:P:32, :], in_=scales_listed[:].bitcast(I32)[8 * r : P : 32, :])
-        ts_listed = {}
-        for c in (1, 0):
-            ts_listed[c] = keep.tile([P, HALF], F32, name="ts_listed%d" % c, align_bytes=64)
-            entries = offsets[:, LIST_COLS * c : LIST_COLS * (c + 1)]
-            nc.vector.tensor_copy(ts_listed[c][:], pool_ts[:].indirect(entries))
+        gather_ts(0, "scales_then_ts")
+
+        ts_cols = {}
+
+        def ts_to_columns(c, tag):
+            bank = psum.tile([P, 2, P], F32, name="ts_bank%d" % c, tag=tag)
+            for u in range(2):
+                nc.tensor.transpose(bank[:, u, :], ts_listed[c][:, u:HALF:2], ident[:])
+            ts_cols[c] = keep.tile([P, 2], F32, name="ts_cols%d" % c)
+            nc.scalar.copy(out=ts_cols[c][:], in_=bank[:, :, TS_ROW])
+
+        ts_to_columns(1, "sum2")
+        ts_rows = psum.tile([P, 2, P], F32, name="ts_rows", tag="sum1")
+        for u in range(2):
+            nc.tensor.transpose(ts_rows[:, u, :], ts_cols[1][:, u : u + 1].to_broadcast([P, P]), ident[:])
 
         q_bf = keep.tile([P, QT, P, PACK], BF16, name="q_bf", align_bytes=64)
         cast_in = q_raw[:].rearrange("p t (s m) -> p s m t", m=QT)
@@ -88,21 +109,12 @@ def tile_attend_tok_idxts_topk_kernel(tc, qT, k_words, k_scales, ts, hw, offs, o
             out=q_words[:].bitcast(FP8X4), scales=q_planes[:], in_=q_bf[:].rearrange("p m s t -> p (m s t)")
         )
 
-        ts_bank = psum.tile([P, 4, P], F32, name="ts_bank", tag="sum2")
-        for c in (1, 0):
-            for u in range(2):
-                nc.tensor.transpose(ts_bank[:, 2 * c + u, :], ts_listed[c][:, u:HALF:2], ident[:])
-        ts_cols = keep.tile([P, 4], F32, name="ts_cols", tag="q_raw_then_ts_cols", align_bytes=64)
-        nc.scalar.copy(out=ts_cols[:], in_=ts_bank[:, :, TS_ROW])
-
-        ts_rows = psum.tile([P, 2, P], F32, name="ts_rows", tag="sum1")
-        for u in range(2):
-            nc.tensor.transpose(ts_rows[:, u, :], ts_cols[:, 2 + u : 3 + u].to_broadcast([P, P]), ident[:])
         hw_ts = []
         for m in range(QT):
             factor = keep.tile([P, 2, P], F32, name="hw_ts%d" % m, align_bytes=64)
             nc.scalar.activation(out=factor[:], in_=ts_rows[:], func=ACT.Copy, scale=hw_cols[:, m : m + 1])
             hw_ts.append(factor)
+        ts_to_columns(0, "sum0")
 
         pe_warm = psum.tile([P, NQ], F32, name="pe_warm", tag="sum2")
         nc.tensor.matmul_mx(
@@ -221,7 +233,7 @@ def tile_attend_tok_idxts_topk_kernel(tc, qT, k_words, k_scales, ts, hw, offs, o
         add_heads(0, total0)
         result0 = keep.tile([P, 2, NPOS], F32, name="result0", align_bytes=64)
         for u in range(2):
-            nc.scalar.activation(out=result0[:, u, :], in_=total0[:, u, :], func=ACT.Copy, scale=ts_cols[:, u : u + 1])
+            nc.scalar.activation(out=result0[:, u, :], in_=total0[:, u, :], func=ACT.Copy, scale=ts_cols[0][:, u : u + 1])
         store(0, result0)
 
         result1 = keep.tile([P, 2, NPOS], F32, name="result1", align_bytes=64)

@@ -27,8 +27,7 @@ QT = NQ // P
 HEADS_LEFT = SEG // QT
 LIST_COLS = HALF // 16
 TS_ROW = P - 1
-SCALAR_CAST = 64
-VECTOR_ZEROES = 1376
+SCALAR_CAST = 58
 
 FLOPS = 2 * N * NQ * D
 BYTES = 4 * D * NQ + D * T + 16 * T + 4 * T + 4 * NQ + 2 * P * (N // 16) + 4 * N * NPOS
@@ -49,13 +48,11 @@ def tile_attend_tok_idxts_topk_kernel(tc, qT, k_words, k_scales, ts, hw, offs, o
         ident = keep.tile([P, P], F32, name="ident", align_bytes=64)
 
         table_seed = keep.tile([P, 1], F32, name="table_seed")
-        nc.vector.memset(pool_scales[:, 0 : T // 8], 0)
-        nc.gpsimd.memset(pool_scales[:, T // 8 : T // 4], 0)
-        nc.gpsimd.memset(table_seed[:], 0.0)
-        nc.gpsimd.memset(pool_ts[0:TS_ROW, VECTOR_ZEROES:T], 0.0)
+        nc.vector.memset(table_seed[:], 0.0)
+        nc.gpsimd.memset(pool_scales[:], 0)
         k_planes = keep.tile([P, N], U8, name="k_planes", align_bytes=64)
         nc.gpsimd.memset(k_planes[:].bitcast(I32), 0)
-        nc.vector.memset(pool_ts[0:TS_ROW, 0:VECTOR_ZEROES], 0.0)
+        nc.vector.memset(pool_ts[0:TS_ROW, :], 0.0)
         make_identity(nc, ident[:])
         table_warm = keep.tile([P, 1], F32, name="table_warm")
         nc.scalar.activation(out=table_warm[:], in_=table_seed[:], func=ACT.Relu)
@@ -77,7 +74,7 @@ def tile_attend_tok_idxts_topk_kernel(tc, qT, k_words, k_scales, ts, hw, offs, o
             entries = offsets[:, LIST_COLS * c : LIST_COLS * (c + 1)]
             nc.vector.tensor_copy(ts_listed[c][:], pool_ts[:].indirect(entries))
 
-        gather_ts(1, "ts_listed1")
+        gather_ts(1, "ts_then_q_bf")
         scales_listed = keep.tile([P, N], U8, name="scales_listed", align_bytes=64)
         nc.vector.tensor_copy(scales_listed[:], pool_scales[:].bitcast(U8).indirect(offsets[:]))
         for r in range(4):
@@ -98,7 +95,7 @@ def tile_attend_tok_idxts_topk_kernel(tc, qT, k_words, k_scales, ts, hw, offs, o
         for u in range(2):
             nc.tensor.transpose(ts_rows[:, u, :], ts_cols[1][:, u : u + 1].to_broadcast([P, P]), ident[:])
 
-        q_bf = keep.tile([P, QT, P, PACK], BF16, name="q_bf", align_bytes=64)
+        q_bf = keep.tile([P, QT, P, PACK], BF16, name="q_bf", tag="ts_then_q_bf", align_bytes=64)
         cast_in = q_raw[:].rearrange("p t (s m) -> p s m t", m=QT)
         cast_out = q_bf[:].rearrange("p m s t -> p s m t")
         nc.scalar.copy(out=cast_out[:, 0:SCALAR_CAST], in_=cast_in[:, 0:SCALAR_CAST])

@@ -27,7 +27,7 @@ QT = NQ // P
 HEADS_LEFT = SEG // QT
 LIST_COLS = HALF // 16
 TS_ROW = P - 1
-SCALAR_CAST = 58
+SCALAR_CAST = 44
 
 FLOPS = 2 * N * NQ * D
 BYTES = 4 * D * NQ + D * T + 16 * T + 4 * T + 4 * NQ + 2 * P * (N // 16) + 4 * N * NPOS
@@ -40,30 +40,32 @@ def tile_attend_tok_idxts_topk_kernel(tc, qT, k_words, k_scales, ts, hw, offs, o
         psum = ctx.enter_context(tc.psum_pool(name="psum", bufs=1))
 
         offsets = keep.tile([P, N // 16], U16, name="offsets")
-        q_raw = keep.tile([P, PACK, NQ], F32, name="q_raw", align_bytes=64)
+        q_raw = keep.tile([P, PACK, NQ], F32, name="q_raw", tag="q_raw_then_ts", align_bytes=64)
         pool_words = keep.tile([P, T], I32, name="pool_words", align_bytes=64)
-        pool_scales = keep.tile([P, T // 4], I32, name="pool_scales", tag="scales_then_ts", align_bytes=64)
+        pool_scales = keep.tile([P, T // 4], I32, name="pool_scales", align_bytes=64)
         pool_ts = keep.tile([P, T], F32, name="pool_ts", align_bytes=64)
         hw_cols = keep.tile([P, QT], F32, name="hw_cols")
         ident = keep.tile([P, P], F32, name="ident", align_bytes=64)
 
         table_seed = keep.tile([P, 1], F32, name="table_seed")
+        nc.vector.memset(pool_scales[:], 0)
         nc.vector.memset(table_seed[:], 0.0)
-        nc.gpsimd.memset(pool_scales[:], 0)
-        k_planes = keep.tile([P, N], U8, name="k_planes", align_bytes=64)
-        nc.gpsimd.memset(k_planes[:].bitcast(I32), 0)
         nc.vector.memset(pool_ts[0:TS_ROW, :], 0.0)
-        make_identity(nc, ident[:])
+        k_planes = keep.tile([P, N], U8, name="k_planes", align_bytes=64)
+        nc.vector.memset(k_planes[:].bitcast(I32), 0)
+        nc.vector.memset(ident[:], 0.0)
+        make_identity(nc, ident[:], nomemset=True)
         table_warm = keep.tile([P, 1], F32, name="table_warm")
         nc.scalar.activation(out=table_warm[:], in_=table_seed[:], func=ACT.Relu)
 
         q_rows = qT[0].rearrange("(p t) q -> p t q", t=PACK)
         scale_rows = k_scales[0].bitcast(I32)
+        nc.sync.dma_start(out=q_raw[:, 0:1, :], in_=q_rows[:, 0:1, :])
         nc.sync.dma_start(offsets[:], offs)
         nc.sync.dma_start(out=pool_ts[TS_ROW:P, :], in_=ts[0:1, :])
-        nc.sync.dma_start(out=q_raw[:, 0:1, :], in_=q_rows[:, 0:1, :])
+        nc.sync.dma_start(out=q_raw[:, 1:2, :], in_=q_rows[:, 1:2, :])
         nc.sync.dma_start(out=pool_scales[0:P:8, :], in_=scale_rows)
-        nc.sync.dma_start(out=q_raw[:, 1:4, :], in_=q_rows[:, 1:4, :])
+        nc.sync.dma_start(out=q_raw[:, 2:4, :], in_=q_rows[:, 2:4, :])
         nc.sync.dma_start(out=hw_cols[:], in_=hw[0, 0].rearrange("(s m) -> s m", m=QT))
         nc.sync.dma_start(out=pool_words[:], in_=k_words[0].rearrange("p n t -> p (n t)").bitcast(I32))
 
@@ -79,7 +81,6 @@ def tile_attend_tok_idxts_topk_kernel(tc, qT, k_words, k_scales, ts, hw, offs, o
         nc.vector.tensor_copy(scales_listed[:], pool_scales[:].bitcast(U8).indirect(offsets[:]))
         for r in range(4):
             nc.sync.dma_start(out=k_planes[:].bitcast(I32)[r:P:32, :], in_=scales_listed[:].bitcast(I32)[8 * r : P : 32, :])
-        gather_ts(0, "scales_then_ts")
 
         ts_cols = {}
 
@@ -100,6 +101,7 @@ def tile_attend_tok_idxts_topk_kernel(tc, qT, k_words, k_scales, ts, hw, offs, o
         cast_out = q_bf[:].rearrange("p m s t -> p s m t")
         nc.scalar.copy(out=cast_out[:, 0:SCALAR_CAST], in_=cast_in[:, 0:SCALAR_CAST])
         nc.vector.tensor_copy(out=cast_out[:, SCALAR_CAST:P], in_=cast_in[:, SCALAR_CAST:P])
+        gather_ts(0, "q_raw_then_ts")
         q_words = keep.tile([P, NQ], U32, name="q_words", align_bytes=64)
         q_planes = keep.tile([P, NQ], U8, name="q_planes", align_bytes=64)
         nc.vector.quantize_mx(
@@ -203,7 +205,9 @@ def tile_attend_tok_idxts_topk_kernel(tc, qT, k_words, k_scales, ts, hw, offs, o
         multiply(1, 1, "score0")
         relu_times_hw_on_vector(2)
         relu_on_scalar(0, 3)
-        relu_on_scalar(1, 0)
+        shared = new_weighted(1, 0)
+        positive_u0 = keep.tile([P, P], F32, name="positive_u0", align_bytes=64)
+        nc.scalar.activation(out=positive_u0[:], in_=scores[(1, 0)][:, 0], func=ACT.Relu)
         multiply(1, 2, "score1")
         multiply(1, 3, "score2")
 
@@ -216,7 +220,8 @@ def tile_attend_tok_idxts_topk_kernel(tc, qT, k_words, k_scales, ts, hw, offs, o
             op1=ALU.add,
         )
         nc.scalar.activation(out=new_weighted(0, 3)[:], in_=positive[(0, 3)][:], func=ACT.Copy, scale=hw_cols[:, 3:4])
-        nc.gpsimd.tensor_tensor(out=new_weighted(1, 0)[:], in0=positive[(1, 0)][:], in1=hw_ts[0][:], op=ALU.mult)
+        nc.gpsimd.tensor_tensor(out=shared[:, 0], in0=positive_u0[:], in1=hw_ts[0][:, 0], op=ALU.mult)
+        relu_times_hw_ts_on_vector(shared[:, 1], scores[(1, 0)][:, 1], hw_ts[0][:, 1])
         for m in (1, 2):
             relu_times_hw_ts_on_vector(new_weighted(1, m)[:], scores[(1, m)], hw_ts[m][:])
         last = new_weighted(1, 3)
@@ -224,7 +229,7 @@ def tile_attend_tok_idxts_topk_kernel(tc, qT, k_words, k_scales, ts, hw, offs, o
             relu_times_hw_ts_on_vector(last[:, u], scores[(1, 3)][:, u], hw_ts[3][:, u])
 
         turn_and_add(0, (2, 1, 3), ("sum0", "score3"))
-        turn_and_add(1, (1, 2, 0, 3), ("sum1", "sum2"))
+        turn_and_add(1, (0, 1, 2, 3), ("sum1", "sum2"))
 
         total0 = keep.tile([P, 2, NPOS], F32, name="total0", align_bytes=64)
         add_heads(0, total0)

@@ -27,7 +27,7 @@ QT = NQ // P
 HEADS_LEFT = SEG // QT
 LIST_COLS = HALF // 16
 TS_ROW = P - 1
-SCALAR_CAST = 44
+SCALAR_CAST = 32
 
 FLOPS = 2 * N * NQ * D
 BYTES = 4 * D * NQ + D * T + 16 * T + 4 * T + 4 * NQ + 2 * P * (N // 16) + 4 * N * NPOS
@@ -40,33 +40,30 @@ def tile_attend_tok_idxts_topk_kernel(tc, qT, k_words, k_scales, ts, hw, offs, o
         psum = ctx.enter_context(tc.psum_pool(name="psum", bufs=1))
 
         offsets = keep.tile([P, N // 16], U16, name="offsets")
-        q_raw = keep.tile([P, PACK, NQ], F32, name="q_raw", tag="q_raw_then_ts", align_bytes=64)
+        q_raw = keep.tile([P, PACK, NQ], F32, name="q_raw", align_bytes=64)
         pool_words = keep.tile([P, T], I32, name="pool_words", align_bytes=64)
         pool_scales = keep.tile([P, T // 4], I32, name="pool_scales", align_bytes=64)
         pool_ts = keep.tile([P, T], F32, name="pool_ts", align_bytes=64)
         hw_cols = keep.tile([P, QT], F32, name="hw_cols")
         ident = keep.tile([P, P], F32, name="ident", align_bytes=64)
 
-        table_seed = keep.tile([P, 1], F32, name="table_seed")
+        zero_col = keep.tile([P, 1], F32, name="zero_col")
         nc.vector.memset(pool_scales[:], 0)
-        nc.vector.memset(table_seed[:], 0.0)
+        nc.vector.memset(zero_col[:], 0.0)
         nc.vector.memset(pool_ts[0:TS_ROW, :], 0.0)
         k_planes = keep.tile([P, N], U8, name="k_planes", align_bytes=64)
         nc.vector.memset(k_planes[:].bitcast(I32), 0)
-        nc.vector.memset(ident[:], 0.0)
+        nc.scalar.activation(out=ident[:], in_=zero_col[:].to_broadcast([P, P]), func=ACT.Copy)
         make_identity(nc, ident[:], nomemset=True)
-        table_warm = keep.tile([P, 1], F32, name="table_warm")
-        nc.scalar.activation(out=table_warm[:], in_=table_seed[:], func=ACT.Relu)
 
         q_rows = qT[0].rearrange("(p t) q -> p t q", t=PACK)
         scale_rows = k_scales[0].bitcast(I32)
         nc.sync.dma_start(out=q_raw[:, 0:1, :], in_=q_rows[:, 0:1, :])
         nc.sync.dma_start(offsets[:], offs)
         nc.sync.dma_start(out=pool_ts[TS_ROW:P, :], in_=ts[0:1, :])
-        nc.sync.dma_start(out=q_raw[:, 1:2, :], in_=q_rows[:, 1:2, :])
-        nc.sync.dma_start(out=pool_scales[0:P:8, :], in_=scale_rows)
-        nc.sync.dma_start(out=q_raw[:, 2:4, :], in_=q_rows[:, 2:4, :])
         nc.sync.dma_start(out=hw_cols[:], in_=hw[0, 0].rearrange("(s m) -> s m", m=QT))
+        nc.sync.dma_start(out=pool_scales[0:P:8, :], in_=scale_rows)
+        nc.sync.dma_start(out=q_raw[:, 1:4, :], in_=q_rows[:, 1:4, :])
         nc.sync.dma_start(out=pool_words[:], in_=k_words[0].rearrange("p n t -> p (n t)").bitcast(I32))
 
         ts_listed = {}
@@ -74,9 +71,10 @@ def tile_attend_tok_idxts_topk_kernel(tc, qT, k_words, k_scales, ts, hw, offs, o
         def gather_ts(c, tag):
             ts_listed[c] = keep.tile([P, HALF], F32, name="ts_listed%d" % c, tag=tag, align_bytes=64)
             entries = offsets[:, LIST_COLS * c : LIST_COLS * (c + 1)]
-            nc.vector.tensor_copy(ts_listed[c][:], pool_ts[:].indirect(entries))
+            nc.scalar.activation(out=ts_listed[c][:], in_=pool_ts[:].indirect(entries), func=ACT.Copy)
 
         gather_ts(1, "ts_then_q_bf")
+        gather_ts(0, "ts_listed0")
         scales_listed = keep.tile([P, N], U8, name="scales_listed", align_bytes=64)
         nc.vector.tensor_copy(scales_listed[:], pool_scales[:].bitcast(U8).indirect(offsets[:]))
         for r in range(4):
@@ -101,7 +99,6 @@ def tile_attend_tok_idxts_topk_kernel(tc, qT, k_words, k_scales, ts, hw, offs, o
         cast_out = q_bf[:].rearrange("p m s t -> p s m t")
         nc.scalar.copy(out=cast_out[:, 0:SCALAR_CAST], in_=cast_in[:, 0:SCALAR_CAST])
         nc.vector.tensor_copy(out=cast_out[:, SCALAR_CAST:P], in_=cast_in[:, SCALAR_CAST:P])
-        gather_ts(0, "q_raw_then_ts")
         q_words = keep.tile([P, NQ], U32, name="q_words", align_bytes=64)
         q_planes = keep.tile([P, NQ], U8, name="q_planes", align_bytes=64)
         nc.vector.quantize_mx(
@@ -115,22 +112,14 @@ def tile_attend_tok_idxts_topk_kernel(tc, qT, k_words, k_scales, ts, hw, offs, o
             hw_ts.append(factor)
         ts_to_columns(0, "sum0")
 
-        pe_warm = psum.tile([P, NQ], F32, name="pe_warm", tag="sum2")
-        nc.tensor.matmul_mx(
-            out=pe_warm[:],
-            lhsT=q_words[:, 0:P].bitcast(FP8X4),
-            lhsT_scale=q_planes[:, 0:P],
-            rhs=q_words[:].bitcast(FP8X4),
-            rhs_scale=q_planes[:],
-            start=True,
-            stop=True,
-        )
-
         k_listed = []
         for c in range(2):
             words = keep.tile([P, HALF], U32, name="k_listed%d" % c, align_bytes=64)
-            entries = offsets[:, LIST_COLS * c : LIST_COLS * (c + 1)]
-            nc.vector.tensor_copy(words[:], pool_words[:].bitcast(U32).indirect(entries))
+            pieces = 2 if c == 0 else 1
+            for g in range(pieces):
+                cols = LIST_COLS // pieces
+                entries = offsets[:, LIST_COLS * c + cols * g : LIST_COLS * c + cols * (g + 1)]
+                nc.vector.tensor_copy(words[:, 16 * cols * g : 16 * cols * (g + 1)], pool_words[:].bitcast(U32).indirect(entries))
             k_listed.append(words)
 
         scores = {}
@@ -138,18 +127,21 @@ def tile_attend_tok_idxts_topk_kernel(tc, qT, k_words, k_scales, ts, hw, offs, o
         weighted = {}
         sums = {}
 
-        def multiply(c, m, tag):
-            bank = psum.tile([P, HALF], F32, name="scores%d%d" % (c, m), tag=tag)
+        banks = {}
+
+        def multiply(c, m, tag, first=0, count=HALF):
+            if first == 0:
+                banks[(c, m)] = psum.tile([P, HALF], F32, name="scores%d%d" % (c, m), tag=tag)
+                scores[(c, m)] = banks[(c, m)][:].rearrange("s (p u) -> s u p", u=2)
             nc.tensor.matmul_mx(
-                out=bank[:],
+                out=banks[(c, m)][:, first : first + count],
                 lhsT=q_words[:, P * m : P * (m + 1)].bitcast(FP8X4),
                 lhsT_scale=q_planes[:, P * m : P * (m + 1)],
-                rhs=k_listed[c][:].bitcast(FP8X4),
-                rhs_scale=k_planes[:, HALF * c : HALF * (c + 1)],
+                rhs=k_listed[c][:, first : first + count].bitcast(FP8X4),
+                rhs_scale=k_planes[:, HALF * c + first : HALF * c + first + count],
                 start=True,
                 stop=True,
             )
-            scores[(c, m)] = bank[:].rearrange("s (p u) -> s u p", u=2)
 
         def new_weighted(c, m):
             tile = keep.tile([P, 2, P], F32, name="weighted%d%d" % (c, m), align_bytes=64)
@@ -174,19 +166,19 @@ def tile_attend_tok_idxts_topk_kernel(tc, qT, k_words, k_scales, ts, hw, offs, o
         def relu_times_hw_ts_on_vector(target, source, factor):
             nc.vector.scalar_tensor_tensor(out=target, in0=source, scalar=0.0, in1=factor, op0=ALU.max, op1=ALU.mult)
 
-        def turn_and_add(c, tiles, tags):
-            for i, m in enumerate(tiles):
-                for u in range(2):
-                    if i == 0:
-                        sums[(c, u)] = psum.tile([P, NPOS, HEADS_LEFT], F32, name="sums%d%d" % (c, u), tag=tags[u])
-                    nc.tensor.matmul(
-                        sums[(c, u)][:].rearrange("p j a -> p (j a)"),
-                        weighted[(c, m)][:, u, :],
-                        ident[:],
-                        start=(i == 0),
-                        stop=(i == len(tiles) - 1),
-                        is_transpose=True,
-                    )
+        def turn_and_add(c, steps, tags):
+            for i, (m, u) in enumerate(steps):
+                first = all(v != u for n, v in steps[:i])
+                if first:
+                    sums[(c, u)] = psum.tile([P, NPOS, HEADS_LEFT], F32, name="sums%d%d" % (c, u), tag=tags[u])
+                nc.tensor.matmul(
+                    sums[(c, u)][:].rearrange("p j a -> p (j a)"),
+                    weighted[(c, m)][:, u, :],
+                    ident[:],
+                    start=first,
+                    stop=all(v != u for n, v in steps[i + 1 :]),
+                    is_transpose=True,
+                )
 
         def add_heads(c, target):
             for u in range(2):
@@ -197,7 +189,10 @@ def tile_attend_tok_idxts_topk_kernel(tc, qT, k_words, k_scales, ts, hw, offs, o
                 out=out[0, HALF * c : HALF * (c + 1), :].rearrange("(p u) j -> p u j", u=2), in_=result[:]
             )
 
-        for m in range(QT):
+        for g in range(2):
+            for m in range(2):
+                multiply(0, m, "score%d" % m, P * g, P)
+        for m in range(2, QT):
             multiply(0, m, "score%d" % m)
         multiply(1, 0, "score4")
         relu_times_hw_on_vector(0)
@@ -222,14 +217,15 @@ def tile_attend_tok_idxts_topk_kernel(tc, qT, k_words, k_scales, ts, hw, offs, o
         nc.scalar.activation(out=new_weighted(0, 3)[:], in_=positive[(0, 3)][:], func=ACT.Copy, scale=hw_cols[:, 3:4])
         nc.gpsimd.tensor_tensor(out=shared[:, 0], in0=positive_u0[:], in1=hw_ts[0][:, 0], op=ALU.mult)
         relu_times_hw_ts_on_vector(shared[:, 1], scores[(1, 0)][:, 1], hw_ts[0][:, 1])
-        for m in (1, 2):
-            relu_times_hw_ts_on_vector(new_weighted(1, m)[:], scores[(1, m)], hw_ts[m][:])
-        last = new_weighted(1, 3)
+        relu_times_hw_ts_on_vector(new_weighted(1, 1)[:], scores[(1, 1)], hw_ts[1][:])
+        for m in (2, 3):
+            new_weighted(1, m)
         for u in range(2):
-            relu_times_hw_ts_on_vector(last[:, u], scores[(1, 3)][:, u], hw_ts[3][:, u])
+            for m in (2, 3):
+                relu_times_hw_ts_on_vector(weighted[(1, m)][:, u], scores[(1, m)][:, u], hw_ts[m][:, u])
 
-        turn_and_add(0, (2, 1, 3), ("sum0", "score3"))
-        turn_and_add(1, (0, 1, 2, 3), ("sum1", "sum2"))
+        turn_and_add(0, [(m, u) for m in (2, 1, 3) for u in range(2)], ("sum0", "score3"))
+        turn_and_add(1, [(m, u) for m in (0, 1) for u in range(2)] + [(m, u) for u in range(2) for m in (2, 3)], ("sum1", "sum2"))
 
         total0 = keep.tile([P, 2, NPOS], F32, name="total0", align_bytes=64)
         add_heads(0, total0)

@@ -27,7 +27,7 @@ QT = NQ // P
 HEADS_LEFT = SEG // QT
 LIST_COLS = HALF // 16
 TS_ROW = P - 1
-SCALAR_CAST = 32
+SCALAR_CAST = 42
 
 FLOPS = 2 * N * NQ * D
 BYTES = 4 * D * NQ + D * T + 16 * T + 4 * T + 4 * NQ + 2 * P * (N // 16) + 4 * N * NPOS
@@ -48,7 +48,7 @@ def tile_attend_tok_idxts_topk_kernel(tc, qT, k_words, k_scales, ts, hw, offs, o
         ident = keep.tile([P, P], F32, name="ident", align_bytes=64)
 
         zero_col = keep.tile([P, 1], F32, name="zero_col")
-        nc.vector.memset(pool_scales[:], 0)
+        nc.gpsimd.memset(pool_scales[:], 0)
         nc.vector.memset(zero_col[:], 0.0)
         nc.vector.memset(pool_ts[0:TS_ROW, :], 0.0)
         k_planes = keep.tile([P, N], U8, name="k_planes", align_bytes=64)
@@ -58,10 +58,10 @@ def tile_attend_tok_idxts_topk_kernel(tc, qT, k_words, k_scales, ts, hw, offs, o
 
         q_rows = qT[0].rearrange("(p t) q -> p t q", t=PACK)
         scale_rows = k_scales[0].bitcast(I32)
+        nc.scalar.dma_start(out=hw_cols[:], in_=hw[0, 0].rearrange("(s m) -> s m", m=QT))
         nc.sync.dma_start(out=q_raw[:, 0:1, :], in_=q_rows[:, 0:1, :])
         nc.sync.dma_start(offsets[:], offs)
         nc.sync.dma_start(out=pool_ts[TS_ROW:P, :], in_=ts[0:1, :])
-        nc.sync.dma_start(out=hw_cols[:], in_=hw[0, 0].rearrange("(s m) -> s m", m=QT))
         nc.sync.dma_start(out=pool_scales[0:P:8, :], in_=scale_rows)
         nc.sync.dma_start(out=q_raw[:, 1:4, :], in_=q_rows[:, 1:4, :])
         nc.sync.dma_start(out=pool_words[:], in_=k_words[0].rearrange("p n t -> p (n t)").bitcast(I32))
@@ -73,7 +73,7 @@ def tile_attend_tok_idxts_topk_kernel(tc, qT, k_words, k_scales, ts, hw, offs, o
             entries = offsets[:, LIST_COLS * c : LIST_COLS * (c + 1)]
             nc.scalar.activation(out=ts_listed[c][:], in_=pool_ts[:].indirect(entries), func=ACT.Copy)
 
-        gather_ts(1, "ts_then_q_bf")
+        gather_ts(1, "ts_listed1")
         gather_ts(0, "ts_listed0")
         scales_listed = keep.tile([P, N], U8, name="scales_listed", align_bytes=64)
         nc.vector.tensor_copy(scales_listed[:], pool_scales[:].bitcast(U8).indirect(offsets[:]))
@@ -94,7 +94,7 @@ def tile_attend_tok_idxts_topk_kernel(tc, qT, k_words, k_scales, ts, hw, offs, o
         for u in range(2):
             nc.tensor.transpose(ts_rows[:, u, :], ts_cols[1][:, u : u + 1].to_broadcast([P, P]), ident[:])
 
-        q_bf = keep.tile([P, QT, P, PACK], BF16, name="q_bf", tag="ts_then_q_bf", align_bytes=64)
+        q_bf = keep.tile([P, QT, P, PACK], BF16, name="q_bf", align_bytes=64)
         cast_in = q_raw[:].rearrange("p t (s m) -> p s m t", m=QT)
         cast_out = q_bf[:].rearrange("p m s t -> p s m t")
         nc.scalar.copy(out=cast_out[:, 0:SCALAR_CAST], in_=cast_in[:, 0:SCALAR_CAST])

@@ -112,6 +112,17 @@ def tile_attend_tok_idxts_topk_kernel(tc, qT, k_words, k_scales, ts, hw, offs, o
             hw_ts.append(factor)
         ts_to_columns(0, "sum0")
 
+        pe_warm = psum.tile([P, HALF], F32, name="pe_warm", tag="sum2")
+        nc.tensor.matmul_mx(
+            out=pe_warm[:],
+            lhsT=q_words[:, 0:P].bitcast(FP8X4),
+            lhsT_scale=q_planes[:, 0:P],
+            rhs=q_words[:, 0:HALF].bitcast(FP8X4),
+            rhs_scale=q_planes[:, 0:HALF],
+            start=True,
+            stop=True,
+        )
+
         k_listed = []
         for c in range(2):
             words = keep.tile([P, HALF], U32, name="k_listed%d" % c, align_bytes=64)

@@ -26,6 +26,7 @@ HALF = N // 2
 QT = NQ // P
 HEADS_LEFT = SEG // QT
 LIST_COLS = HALF // 16
+HW_ROW = P // 2 - 1
 TS_ROW = P - 1
 SCALAR_CAST = 42
 
@@ -51,6 +52,9 @@ def tile_attend_tok_idxts_topk_kernel(tc, qT, k_words, k_scales, ts, hw, offs, o
         nc.gpsimd.memset(pool_scales[:], 0)
         nc.vector.memset(zero_col[:], 0.0)
         nc.vector.memset(pool_ts[0:TS_ROW, :], 0.0)
+        hw_row = keep.tile([P, NQ], F32, name="hw_row", align_bytes=64)
+        nc.vector.memset(hw_row[0:HW_ROW, :], 0.0)
+        nc.vector.memset(hw_row[HW_ROW + 1 : P, :], 0.0)
         k_planes = keep.tile([P, N], U8, name="k_planes", align_bytes=64)
         nc.vector.memset(k_planes[:].bitcast(I32), 0)
         nc.scalar.activation(out=ident[:], in_=zero_col[:].to_broadcast([P, P]), func=ACT.Copy)
@@ -58,13 +62,18 @@ def tile_attend_tok_idxts_topk_kernel(tc, qT, k_words, k_scales, ts, hw, offs, o
 
         q_rows = qT[0].rearrange("(p t) q -> p t q", t=PACK)
         scale_rows = k_scales[0].bitcast(I32)
-        nc.scalar.dma_start(out=hw_cols[:], in_=hw[0, 0].rearrange("(s m) -> s m", m=QT))
         nc.sync.dma_start(out=q_raw[:, 0:1, :], in_=q_rows[:, 0:1, :])
         nc.sync.dma_start(offsets[:], offs)
         nc.sync.dma_start(out=pool_ts[TS_ROW:P, :], in_=ts[0:1, :])
+        nc.sync.dma_start(out=hw_row[HW_ROW : HW_ROW + 1, :], in_=hw[0])
         nc.sync.dma_start(out=pool_scales[0:P:8, :], in_=scale_rows)
         nc.sync.dma_start(out=q_raw[:, 1:4, :], in_=q_rows[:, 1:4, :])
         nc.sync.dma_start(out=pool_words[:], in_=k_words[0].rearrange("p n t -> p (n t)").bitcast(I32))
+
+        hw_bank = psum.tile([P, QT, P], F32, name="hw_bank", tag="score4")
+        for m in range(QT):
+            nc.tensor.transpose(hw_bank[:, m, :], hw_row[:, m:NQ:QT], ident[:])
+        nc.scalar.copy(out=hw_cols[:], in_=hw_bank[:, :, HW_ROW])
 
         ts_listed = {}
 

@@ -30,6 +30,8 @@ HW_ROW = P // 2 - 1
 TS_ROW = P - 1
 SCALAR_CAST = 42
 
+Q_FIRST = 640
+
 FLOPS = 2 * N * NQ * D
 BYTES = 4 * D * NQ + D * T + 16 * T + 4 * T + 4 * NQ + 2 * P * (N // 16) + 4 * N * NPOS
 
@@ -60,14 +62,15 @@ def tile_attend_tok_idxts_topk_kernel(tc, qT, k_words, k_scales, ts, hw, offs, o
         nc.scalar.activation(out=ident[:], in_=zero_col[:].to_broadcast([P, P]), func=ACT.Copy)
         make_identity(nc, ident[:], nomemset=True)
 
-        q_rows = qT[0].rearrange("(p t) q -> p t q", t=PACK)
+        q_rows = qT[0].rearrange("(p t) q -> p (t q)", t=PACK)
+        q_flat = q_raw[:].rearrange("p t q -> p (t q)")
         scale_rows = k_scales[0].bitcast(I32)
-        nc.sync.dma_start(out=q_raw[:, 0:1, :], in_=q_rows[:, 0:1, :])
+        nc.sync.dma_start(out=q_flat[:, 0:Q_FIRST], in_=q_rows[:, 0:Q_FIRST])
         nc.sync.dma_start(offsets[:], offs)
         nc.sync.dma_start(out=pool_ts[TS_ROW:P, :], in_=ts[0:1, :])
         nc.sync.dma_start(out=hw_row[HW_ROW : HW_ROW + 1, :], in_=hw[0])
         nc.sync.dma_start(out=pool_scales[0:P:8, :], in_=scale_rows)
-        nc.sync.dma_start(out=q_raw[:, 1:4, :], in_=q_rows[:, 1:4, :])
+        nc.sync.dma_start(out=q_flat[:, Q_FIRST : PACK * NQ], in_=q_rows[:, Q_FIRST : PACK * NQ])
         nc.sync.dma_start(out=pool_words[:], in_=k_words[0].rearrange("p n t -> p (n t)").bitcast(I32))
 
         hw_bank = psum.tile([P, QT, P], F32, name="hw_bank", tag="score4")

from contextlib import ExitStack

import concourse.mybir as mybir
from concourse.masks import make_identity

F32 = mybir.dt.float32
BF16 = mybir.dt.bfloat16
I32 = mybir.dt.int32
U32 = mybir.dt.uint32
U16 = mybir.dt.uint16
U8 = mybir.dt.uint8
FP8X4 = mybir.dt.float8_e4m3fn_x4
ALU = mybir.AluOpType
ACT = mybir.ActivationFunctionType
AXIS_X = mybir.AxisListType.X

P = 128
PACK = 4
T = 2048
N = 512
NQ = 512
D = 512
SEG = 16
NPOS = NQ // SEG
HALF = N // 2
QT = NQ // P
HEADS_LEFT = SEG // QT
LIST_COLS = HALF // 16
HW_ROW = P // 2 - 1
TS_ROW = P - 1
SCALAR_CAST = 42

Q_FIRST = 640

FLOPS = 2 * N * NQ * D
BYTES = 4 * D * NQ + D * T + 16 * T + 4 * T + 4 * NQ + 2 * P * (N // 16) + 4 * N * NPOS


def tile_attend_tok_idxts_topk_kernel(tc, qT, k_words, k_scales, ts, hw, offs, out):
    nc = tc.nc
    with ExitStack() as ctx:
        keep = ctx.enter_context(tc.tile_pool(name="keep", bufs=1))
        psum = ctx.enter_context(tc.psum_pool(name="psum", bufs=1))

        offsets = keep.tile([P, N // 16], U16, name="offsets")
        q_raw = keep.tile([P, PACK, NQ], F32, name="q_raw", align_bytes=64)
        pool_words = keep.tile([P, T], I32, name="pool_words", align_bytes=64)
        pool_scales = keep.tile([P, T // 4], I32, name="pool_scales", align_bytes=64)
        pool_ts = keep.tile([P, T], F32, name="pool_ts", align_bytes=64)
        hw_cols = keep.tile([P, QT], F32, name="hw_cols")
        ident = keep.tile([P, P], F32, name="ident", align_bytes=64)

        zero_col = keep.tile([P, 1], F32, name="zero_col")
        nc.gpsimd.memset(pool_scales[:], 0)
        nc.vector.memset(zero_col[:], 0.0)
        nc.vector.memset(pool_ts[0:TS_ROW, :], 0.0)
        hw_row = keep.tile([P, NQ], F32, name="hw_row", align_bytes=64)
        nc.vector.memset(hw_row[0:HW_ROW, :], 0.0)
        nc.vector.memset(hw_row[HW_ROW + 1 : P, :], 0.0)
        k_planes = keep.tile([P, N], U8, name="k_planes", align_bytes=64)
        nc.vector.memset(k_planes[:].bitcast(I32), 0)
        nc.scalar.activation(out=ident[:], in_=zero_col[:].to_broadcast([P, P]), func=ACT.Copy)
        make_identity(nc, ident[:], nomemset=True)

        q_rows = qT[0].rearrange("(p t) q -> p (t q)", t=PACK)
        q_flat = q_raw[:].rearrange("p t q -> p (t q)")
        scale_rows = k_scales[0].bitcast(I32)
        nc.sync.dma_start(out=q_flat[:, 0:Q_FIRST], in_=q_rows[:, 0:Q_FIRST])
        nc.sync.dma_start(offsets[:], offs)
        nc.sync.dma_start(out=pool_ts[TS_ROW:P, :], in_=ts[0:1, :])
        nc.sync.dma_start(out=hw_row[HW_ROW : HW_ROW + 1, :], in_=hw[0])
        nc.sync.dma_start(out=pool_scales[0:P:8, :], in_=scale_rows)
        nc.sync.dma_start(out=q_flat[:, Q_FIRST : PACK * NQ], in_=q_rows[:, Q_FIRST : PACK * NQ])
        nc.sync.dma_start(out=pool_words[:], in_=k_words[0].rearrange("p n t -> p (n t)").bitcast(I32))

        hw_bank = psum.tile([P, QT, P], F32, name="hw_bank", tag="score4")
        for m in range(QT):
            nc.tensor.transpose(hw_bank[:, m, :], hw_row[:, m:NQ:QT], ident[:])
        nc.scalar.copy(out=hw_cols[:], in_=hw_bank[:, :, HW_ROW])

        ts_listed = {}

        def gather_ts(c, tag):
            ts_listed[c] = keep.tile([P, HALF], F32, name="ts_listed%d" % c, tag=tag, align_bytes=64)
            entries = offsets[:, LIST_COLS * c : LIST_COLS * (c + 1)]
            nc.scalar.activation(out=ts_listed[c][:], in_=pool_ts[:].indirect(entries), func=ACT.Copy)

        gather_ts(1, "ts_listed1")
        gather_ts(0, "ts_listed0")
        scales_listed = keep.tile([P, N], U8, name="scales_listed", align_bytes=64)
        nc.vector.tensor_copy(scales_listed[:], pool_scales[:].bitcast(U8).indirect(offsets[:]))
        for r in range(4):
            nc.sync.dma_start(out=k_planes[:].bitcast(I32)[r:P:32, :], in_=scales_listed[:].bitcast(I32)[8 * r : P : 32, :])

        ts_cols = {}

        def ts_to_columns(c, tag):
            bank = psum.tile([P, 2, P], F32, name="ts_bank%d" % c, tag=tag)
            for u in range(2):
                nc.tensor.transpose(bank[:, u, :], ts_listed[c][:, u:HALF:2], ident[:])
            ts_cols[c] = keep.tile([P, 2], F32, name="ts_cols%d" % c)
            nc.scalar.copy(out=ts_cols[c][:], in_=bank[:, :, TS_ROW])

        ts_to_columns(1, "sum2")
        ts_rows = psum.tile([P, 2, P], F32, name="ts_rows", tag="sum1")
        for u in range(2):
            nc.tensor.transpose(ts_rows[:, u, :], ts_cols[1][:, u : u + 1].to_broadcast([P, P]), ident[:])

        q_bf = keep.tile([P, QT, P, PACK], BF16, name="q_bf", align_bytes=64)
        cast_in = q_raw[:].rearrange("p t (s m) -> p s m t", m=QT)
        cast_out = q_bf[:].rearrange("p m s t -> p s m t")
        nc.scalar.copy(out=cast_out[:, 0:SCALAR_CAST], in_=cast_in[:, 0:SCALAR_CAST])
        nc.vector.tensor_copy(out=cast_out[:, SCALAR_CAST:P], in_=cast_in[:, SCALAR_CAST:P])
        q_words = keep.tile([P, NQ], U32, name="q_words", align_bytes=64)
        q_planes = keep.tile([P, NQ], U8, name="q_planes", align_bytes=64)
        nc.vector.quantize_mx(
            out=q_words[:].bitcast(FP8X4), scales=q_planes[:], in_=q_bf[:].rearrange("p m s t -> p (m s t)")
        )

        hw_ts = []
        for m in range(QT):
            factor = keep.tile([P, 2, P], F32, name="hw_ts%d" % m, align_bytes=64)
            nc.scalar.activation(out=factor[:], in_=ts_rows[:], func=ACT.Copy, scale=hw_cols[:, m : m + 1])
            hw_ts.append(factor)
        ts_to_columns(0, "sum0")

        pe_warm = psum.tile([P, HALF], F32, name="pe_warm", tag="sum2")
        nc.tensor.matmul_mx(
            out=pe_warm[:],
            lhsT=q_words[:, 0:P].bitcast(FP8X4),
            lhsT_scale=q_planes[:, 0:P],
            rhs=q_words[:, 0:HALF].bitcast(FP8X4),
            rhs_scale=q_planes[:, 0:HALF],
            start=True,
            stop=True,
        )

        k_listed = []
        for c in range(2):
            words = keep.tile([P, HALF], U32, name="k_listed%d" % c, align_bytes=64)
            pieces = 2 if c == 0 else 1
            for g in range(pieces):
                cols = LIST_COLS // pieces
                entries = offsets[:, LIST_COLS * c + cols * g : LIST_COLS * c + cols * (g + 1)]
                nc.vector.tensor_copy(words[:, 16 * cols * g : 16 * cols * (g + 1)], pool_words[:].bitcast(U32).indirect(entries))
            k_listed.append(words)

        scores = {}
        positive = {}
        weighted = {}
        sums = {}

        banks = {}

        def multiply(c, m, tag, first=0, count=HALF):
            if first == 0:
                banks[(c, m)] = psum.tile([P, HALF], F32, name="scores%d%d" % (c, m), tag=tag)
                scores[(c, m)] = banks[(c, m)][:].rearrange("s (p u) -> s u p", u=2)
            nc.tensor.matmul_mx(
                out=banks[(c, m)][:, first : first + count],
                lhsT=q_words[:, P * m : P * (m + 1)].bitcast(FP8X4),
                lhsT_scale=q_planes[:, P * m : P * (m + 1)],
                rhs=k_listed[c][:, first : first + count].bitcast(FP8X4),
                rhs_scale=k_planes[:, HALF * c + first : HALF * c + first + count],
                start=True,
                stop=True,
            )

        def new_weighted(c, m):
            tile = keep.tile([P, 2, P], F32, name="weighted%d%d" % (c, m), align_bytes=64)
            weighted[(c, m)] = tile
            return tile

        def relu_on_scalar(c, m):
            tile = keep.tile([P, 2, P], F32, name="positive%d%d" % (c, m), align_bytes=64)
            nc.scalar.activation(out=tile[:], in_=scores[(c, m)], func=ACT.Relu)
            positive[(c, m)] = tile

        def relu_times_hw_on_vector(m):
            nc.vector.tensor_scalar(
                out=new_weighted(0, m)[:],
                in0=scores[(0, m)],
                scalar1=0.0,
                scalar2=hw_cols[:, m : m + 1],
                op0=ALU.max,
                op1=ALU.mult,
            )

        def relu_times_hw_ts_on_vector(target, source, factor):
            nc.vector.scalar_tensor_tensor(out=target, in0=source, scalar=0.0, in1=factor, op0=ALU.max, op1=ALU.mult)

        def turn_and_add(c, steps, tags):
            for i, (m, u) in enumerate(steps):
                first = all(v != u for n, v in steps[:i])
                if first:
                    sums[(c, u)] = psum.tile([P, NPOS, HEADS_LEFT], F32, name="sums%d%d" % (c, u), tag=tags[u])
                nc.tensor.matmul(
                    sums[(c, u)][:].rearrange("p j a -> p (j a)"),
                    weighted[(c, m)][:, u, :],
                    ident[:],
                    start=first,
                    stop=all(v != u for n, v in steps[i + 1 :]),
                    is_transpose=True,
                )

        def add_heads(c, target):
            for u in range(2):
                nc.vector.tensor_reduce(out=target[:, u, :], in_=sums[(c, u)][:], axis=AXIS_X, op=ALU.add)

        def store(c, result):
            nc.sync.dma_start(
                out=out[0, HALF * c : HALF * (c + 1), :].rearrange("(p u) j -> p u j", u=2), in_=result[:]
            )

        for g in range(2):
            for m in range(2):
                multiply(0, m, "score%d" % m, P * g, P)
        for m in range(2, QT):
            multiply(0, m, "score%d" % m)
        multiply(1, 0, "score4")
        relu_times_hw_on_vector(0)
        relu_on_scalar(0, 1)
        multiply(1, 1, "score0")
        relu_times_hw_on_vector(2)
        relu_on_scalar(0, 3)
        shared = new_weighted(1, 0)
        positive_u0 = keep.tile([P, P], F32, name="positive_u0", align_bytes=64)
        nc.scalar.activation(out=positive_u0[:], in_=scores[(1, 0)][:, 0], func=ACT.Relu)
        multiply(1, 2, "score1")
        multiply(1, 3, "score2")

        nc.vector.scalar_tensor_tensor(
            out=new_weighted(0, 1)[:],
            in0=positive[(0, 1)][:],
            scalar=hw_cols[:, 1:2],
            in1=weighted[(0, 0)][:],
            op0=ALU.mult,
            op1=ALU.add,
        )
        nc.scalar.activation(out=new_weighted(0, 3)[:], in_=positive[(0, 3)][:], func=ACT.Copy, scale=hw_cols[:, 3:4])
        nc.gpsimd.tensor_tensor(out=shared[:, 0], in0=positive_u0[:], in1=hw_ts[0][:, 0], op=ALU.mult)
        relu_times_hw_ts_on_vector(shared[:, 1], scores[(1, 0)][:, 1], hw_ts[0][:, 1])
        relu_times_hw_ts_on_vector(new_weighted(1, 1)[:], scores[(1, 1)], hw_ts[1][:])
        for m in (2, 3):
            new_weighted(1, m)
        for u in range(2):
            for m in (2, 3):
                relu_times_hw_ts_on_vector(weighted[(1, m)][:, u], scores[(1, m)][:, u], hw_ts[m][:, u])

        turn_and_add(0, [(m, u) for m in (2, 1, 3) for u in range(2)], ("sum0", "score3"))
        turn_and_add(1, [(m, u) for m in (0, 1) for u in range(2)] + [(m, u) for u in range(2) for m in (2, 3)], ("sum1", "sum2"))

        total0 = keep.tile([P, 2, NPOS], F32, name="total0", align_bytes=64)
        add_heads(0, total0)
        result0 = keep.tile([P, 2, NPOS], F32, name="result0", align_bytes=64)
        for u in range(2):
            nc.scalar.activation(out=result0[:, u, :], in_=total0[:, u, :], func=ACT.Copy, scale=ts_cols[0][:, u : u + 1])
        store(0, result0)

        result1 = keep.tile([P, 2, NPOS], F32, name="result1", align_bytes=64)
        add_heads(1, result1)
        store(1, result1)
